import numpy as np
import ml_dtypes


def mxq(x, axis, fmt="e4m3"):
    dtype, down = {"e4m3": (ml_dtypes.float8_e4m3fn, 7), "e5m2": (ml_dtypes.float8_e5m2, 14)}[fmt]
    v = np.moveaxis(np.asarray(x, np.float32).astype(ml_dtypes.bfloat16).astype(np.float64), axis, -1)
    blocks = v.reshape(v.shape[:-1] + (-1, 32))
    amax = np.abs(blocks).max(-1, keepdims=True)
    byte = np.maximum(np.where(amax > 0, np.frexp(amax)[1] - 1 + 127, 0) - down, 1)
    scale = np.exp2(byte - 127.0)
    codes = (blocks / scale).astype(np.float32).astype(dtype).astype(np.float64)
    return np.moveaxis((codes * scale).reshape(v.shape), -1, axis)


WIDE = False


def mx_kscale(k):
    if not WIDE:
        return np.ones(k)
    levels = np.array([10, -10, 5, -5, 0])
    if k % 512:
        return np.exp2(np.random.permutation(np.resize(levels, k // 32))).repeat(32)
    a = np.empty((k // 512, 16))
    for p in range(k // 512):
        a[p, :8] = np.random.permutation(np.resize(levels, 8))
        for g in range(8):
            far = levels[np.abs(levels - a[p, g]) >= 10]
            a[p, g + 8] = far[np.random.randint(len(far))]
    return np.exp2(a.ravel()).repeat(32)


def f64(x):
    return np.asarray(x).astype(np.float64)


def striped(idx):
    return np.tile(idx.reshape(-1, 16).T, (8, 1)).astype(np.uint16)


def unstriped(offs):
    return offs[:16].T.reshape(-1).astype(np.int64)


E2M1 = np.array([0.0, 0.5, 1.0, 1.5, 2.0, 3.0, 4.0, 6.0, -0.0, -0.5, -1.0, -1.5, -2.0, -3.0, -4.0, -6.0])


def pack_weight(w, fmt):
    k, n = w.shape
    w = f64(np.asarray(w, np.float32).astype(ml_dtypes.bfloat16)).reshape(k // 32, 32, n)
    amax = np.abs(w).max(1)
    if fmt == "e4m3":
        byte = np.frexp(amax)[1] - 1 + 127 - 7
    else:
        mant, ex = np.frexp(amax / 6.0)
        byte = np.where(mant > 0.5, ex, ex - 1) + 127
    byte = np.clip(np.where(amax > 0, byte, 1), 1, 254)
    scaled = (w * np.exp2(127.0 - byte)[:, None, :]).reshape(k, n).astype(np.float32)
    by_word = np.ascontiguousarray(scaled.reshape(k // 512, 128, 4, n).transpose(0, 1, 3, 2))
    if fmt == "e4m3":
        words = by_word.astype(ml_dtypes.float8_e4m3fn).view(np.uint8)
    else:
        c = by_word.astype(ml_dtypes.float4_e2m1fn).view(np.uint8) & 0xF
        words = (c[..., 0::2] | (c[..., 1::2] << 4)).reshape(k // 512, 128, 2 * n)
    return np.ascontiguousarray(words), np.ascontiguousarray(byte.astype(np.uint8).reshape(k // 512, 16, n))


def unpack_weight(words, scales, fmt):
    g, _, n = scales.shape
    words = np.ascontiguousarray(words).reshape(g, 128, n, -1)
    if fmt == "e4m3":
        vals = words.view(ml_dtypes.float8_e4m3fn).astype(np.float64)
    else:
        nib = np.empty((g, 128, n, 4), np.uint8)
        nib[..., 0::2] = words & 0xF
        nib[..., 1::2] = words >> 4
        vals = E2M1[nib]
    vals = vals * np.repeat(np.exp2(scales.astype(np.float64) - 127.0), 8, axis=1)[..., None]
    return vals.transpose(0, 1, 3, 2).reshape(g * 512, n)


def gelu(v):
    return 0.5 * v * (1.0 + np.tanh(np.sqrt(2.0 / np.pi) * (v + 0.044715 * v**3)))


def pack_table4(v):
    words, scales = pack_weight(v, "e2m1")
    g, t = words.shape[0] // 2, v.shape[1]
    words = words.reshape(g, 2, 128, t, 2).transpose(0, 2, 3, 1, 4)
    return np.concatenate([words.reshape(g, -1), scales.reshape(g, -1)], axis=1)


def unpack_table4(tab):
    g, t = tab.shape[0], tab.shape[1] // 544
    words = tab[:, :512 * t].reshape(g, 128, t, 2, 2).transpose(0, 3, 1, 2, 4).reshape(2 * g, 128, 2 * t)
    return unpack_weight(words, tab[:, 512 * t:].reshape(2 * g, 16, t), "e2m1")


K, T, S, H, N = 1024, 4096, 1024, 1024, 512

def setup_inputs():
    n = np.random.standard_normal
    s = mx_kscale(K)[:, None]
    u = mx_kscale(H)[:, None]
    tab = pack_table4(n((K, T)) * s)
    offs = striped(np.random.permutation(T)[:S])
    we = (n((K, H)) / np.sqrt(K) / s).astype(np.float32)
    wb_words, wb_scales = pack_weight(0.5 * n((K, H)) / np.sqrt(K) / s * u.T, "e2m1")
    gain = (np.exp(0.3 * n(H)) * u[:, 0]).astype(np.float32)
    w2_words, w2_scales = pack_weight(n((H, N)) / np.sqrt(H) / u, "e4m3")
    return {"tab": tab, "offs": offs, "we": we,
            "wb_words": wb_words, "wb_scales": wb_scales, "gain": gain,
            "w2_words": w2_words, "w2_scales": w2_scales}

def reference(tab, offs, we, wb_words, wb_scales, gain, w2_words, w2_scales):
    v = unpack_table4(tab)[:, unstriped(offs)]
    weq = mxq(f64(we), 0, "e4m3")
    wb = unpack_weight(wb_words, wb_scales, "e2m1")
    w2 = unpack_weight(w2_words, w2_scales, "e4m3")
    e = weq.T @ v
    b = wb.T @ v
    h = f64(gain)[:, None] * np.log(1.0 + np.abs(e)) - b
    hq = mxq(h, 0, "e4m3")
    out = w2.T @ hq
    return out

@@ -1,0 +1,295 @@
+from contextlib import ExitStack
+
+import concourse.mybir as mybir
+
+K, T, S, H, N = 1024, 4096, 1024, 1024, 512
+FLOPS = 2 * (2 * K * H * S + H * N * S)
+
+F32 = mybir.dt.float32
+BF16 = mybir.dt.bfloat16
+I32 = mybir.dt.int32
+U32 = mybir.dt.uint32
+U16 = mybir.dt.uint16
+U8 = mybir.dt.uint8
+FP8X4 = mybir.dt.float8_e4m3fn_x4
+FP4X4 = mybir.dt.float4_e2m1fn_x4
+ACT = mybir.ActivationFunctionType
+ALU = mybir.AluOpType
+
+P = 128
+W = 512
+ROWS = 32
+V_AT, WB_AT, PLANE = 0, S, S + H
+
+
+def tile_list_barcode_programme_scores_kernel(
+    tc, tab, offs, we, wb_words, wb_scales, gain, w2_words, w2_scales, out
+):
+    nc = tc.nc
+    with ExitStack() as ctx:
+        keep = ctx.enter_context(tc.tile_pool(name="keep", bufs=1))
+        ring = ctx.enter_context(tc.tile_pool(name="ring", bufs=2))
+        reuse = ctx.enter_context(tc.tile_pool(name="reuse", bufs=1))
+        psum = ctx.enter_context(tc.psum_pool(name="psum", bufs=1))
+
+        def bank(i, name):
+            return psum.tile([P, W], F32, name=name, tag="bank%d" % i)
+
+        offsets = keep.tile([P, S // 16], U16, name="offsets")
+        scale_win = keep.tile([P, T // 4], I32, name="scale_win", align_bytes=64)
+        word_win = reuse.tile([P, T], I32, name="word_win", align_bytes=64, offset=0)
+        planes = keep.tile([P, 2, PLANE // 4], I32, name="planes", align_bytes=64)
+        rows = keep.tile([P, PLANE // 4], I32, name="rows", align_bytes=64)
+        wb_rows = keep.tile([P, H // 4], I32, name="wb_rows", align_bytes=64)
+        gain_sb = keep.tile([P, 2, 4], F32, name="gain_sb")
+        warm = keep.tile([P, 1], F32, name="warm")
+        warm_out = keep.tile([P, 1], F32, name="warm_out")
+
+        nc.vector.memset(warm[:], 1.0)
+        nc.scalar.activation(out=warm_out[:], in_=warm[:], func=ACT.Ln)
+        nc.vector.memset(wb_rows[32:64, :], 0)
+        nc.vector.memset(wb_rows[64:128, :], 0)
+        nc.vector.memset(scale_win[32:64, :], 0)
+        nc.vector.memset(scale_win[64:128, :], 0)
+        nc.vector.memset(planes[:], 0)
+
+        nc.sync.dma_start(
+            out=scale_win[0:ROWS, :],
+            in_=tab[0, 512 * T : 544 * T].rearrange("(r b) -> r b", r=ROWS).bitcast(I32),
+        )
+        nc.sync.dma_start(offsets[:], offs)
+        nc.sync.dma_start(out=wb_rows[0:ROWS, :], in_=wb_scales.rearrange("g q c -> (g q) c").bitcast(I32))
+
+        def load_wb(a):
+            raw = reuse.tile([P, 2, W // 2], I32, name="wb_raw%d" % a, align_bytes=64, offset=20480 + 1024 * a)
+            nc.sync.dma_start(
+                out=raw[:],
+                in_=wb_words[:, :, 2 * W * a : 2 * W * (a + 1)].rearrange("g p b -> p g b").bitcast(I32),
+            )
+            return raw
+
+        wb_raw = {0: load_wb(0)}
+        nc.sync.dma_start(
+            out=word_win[:], in_=tab[0, 0 : 512 * T].rearrange("(p b) -> p b", p=P).bitcast(I32)
+        )
+
+        chunks = [(0, 0, 512), (1, 0, 256), (1, 256, 256)]
+
+        def load_we(a):
+            raws = []
+            for i, (g, c0, cw) in enumerate(chunks):
+                raw = keep.tile([P, 4, cw], F32, name="we_raw%d_%d" % (a, i), tag="we_raw%d" % i)
+                nc.sync.dma_start(
+                    out=raw[:],
+                    in_=we[W * g : W * (g + 1), W * a + c0 : W * a + c0 + cw].rearrange("(p j) c -> p j c", j=4),
+                )
+                raws.append(raw)
+            return raws
+
+        we_raw = {0: load_we(0)}
+        nc.gpsimd.dma_start(out=gain_sb[:], in_=gain.rearrange("(a p t) -> p a t", a=2, t=4))
+
+        nc.vector.tensor_copy(
+            out=rows[:].bitcast(U8)[:, WB_AT:PLANE].rearrange("p (a t m) -> p a t m", a=2, t=4),
+            in_=wb_rows[:].bitcast(U8).rearrange("p (a m t) -> p a t m", a=2, t=4),
+        )
+        picked_scales = keep.tile([P, S], U8, name="picked_scales", align_bytes=64)
+        nc.vector.tensor_copy(picked_scales[:], scale_win[:].bitcast(U8).indirect(offsets[:]))
+        nc.vector.tensor_copy(out=rows[:, 0 : S // 4], in_=picked_scales[:].bitcast(I32))
+        for g in range(2):
+            queue = nc.scalar if g == 0 else nc.gpsimd
+            for q in range(4):
+                queue.dma_start(
+                    out=planes[32 * q : 32 * q + 4, g, :], in_=rows[16 * g + 4 * q : 16 * g + 4 * q + 4, :]
+                )
+        plane_bytes = planes[:].bitcast(U8)
+
+        wb_codes = {}
+
+        def permute_wb(a):
+            codes = reuse.tile([P, 2, 2 * W], U8, name="wb_codes%d" % a, align_bytes=64, offset=(24576, 6144)[a])
+            nc.vector.tensor_copy(
+                out=codes[:].bitcast(U16).rearrange("p g (t m) -> p g t m", t=4),
+                in_=wb_raw[a][:].bitcast(U16).rearrange("p g (m t) -> p g t m", t=4),
+            )
+            wb_codes[a] = codes
+
+        permute_wb(0)
+        wb_raw[1] = load_wb(1)
+
+        v_codes = {}
+        for jt in range(2):
+            picked = keep.tile([P, W], U32, name="picked_words%d" % jt, align_bytes=64)
+            nc.vector.tensor_copy(
+                picked[:], word_win[:].bitcast(U32).indirect(offsets[:, 32 * jt : 32 * (jt + 1)])
+            )
+            codes = keep.tile([P, 2, 2 * W], U8, name="v_codes%d" % jt, align_bytes=64)
+            nc.vector.tensor_copy(
+                out=codes[:].bitcast(U16), in_=picked[:].bitcast(U16).rearrange("p (n g) -> p g n", g=2)
+            )
+            v_codes[jt] = codes
+
+        we_bf, we_codes, we_scales = {}, {}, {}
+        for a in range(2):
+            for g in range(2):
+                bf_at = {(0, 0): 17408, (0, 1): 0, (1, 0): 28672, (1, 1): 32768}[a, g]
+                codes_at = {(0, 0): 4096, (0, 1): 36864, (1, 0): 38912, (1, 1): 40960}[a, g]
+                we_bf[a, g] = reuse.tile([P, 4 * W], BF16, name="we_bf%d%d" % (a, g), align_bytes=64, offset=bf_at)
+                we_codes[a, g] = reuse.tile([P, W], U32, name="we_codes%d%d" % (a, g), align_bytes=64, offset=codes_at)
+                we_scales[a, g] = keep.tile([P, W], U8, name="we_scales%d%d" % (a, g), align_bytes=64)
+
+        def round_we(engine, a, i, m0, m1):
+            g, c0 = chunks[i][0], chunks[i][1]
+            dst = we_bf[a, g][:].rearrange("p (t m j) -> p m j t", t=4, j=4)[:, c0 // 4 + m0 : c0 // 4 + m1]
+            src = we_raw[a][i][:].rearrange("p j (m t) -> p m j t", t=4)[:, m0:m1]
+            if engine == "scalar":
+                nc.scalar.copy(out=dst, in_=src)
+            else:
+                nc.vector.tensor_copy(out=dst, in_=src)
+
+        def quantise_we(a, g, t0, t1):
+            nc.vector.quantize_mx(
+                out=we_codes[a, g][:, P * t0 : P * t1].bitcast(FP8X4),
+                scales=we_scales[a, g][:, P * t0 : P * t1],
+                in_=we_bf[a, g][:, W * t0 : W * t1],
+            )
+
+        round_we("scalar", 0, 0, 0, 128)
+        quantise_we(0, 0, 0, 4)
+        round_we("vector", 0, 1, 0, 64)
+        round_we("vector", 0, 2, 0, 40)
+        round_we("scalar", 0, 2, 40, 64)
+        for t in range(4):
+            quantise_we(0, 1, t, t + 1)
+        permute_wb(1)
+        we_raw[1] = load_we(1)
+        w2_codes = reuse.tile([P, 2, N], I32, name="w2_codes", align_bytes=64, offset=0)
+        nc.sync.dma_start(out=w2_codes[:], in_=w2_words.rearrange("a p c i -> p a (c i)").bitcast(I32))
+        w2_planes = reuse.tile([P, 2, N // 4], I32, name="w2_planes", align_bytes=64, offset=17408)
+        nc.vector.memset(w2_planes[:], 0)
+        for q in range(4):
+            nc.sync.dma_start(
+                out=w2_planes[32 * q : 32 * q + 4, :, :],
+                in_=w2_scales[:, 4 * q : 4 * q + 4, :].rearrange("a r c -> r a c").bitcast(I32),
+            )
+        w2_plane_bytes = w2_planes[:].bitcast(U8)
+
+        later = {
+            0: [lambda: round_we("vector", 1, 0, 0, 64)],
+            1: [lambda: round_we("vector", 1, 0, 64, 128)],
+            2: [lambda: quantise_we(1, 0, 0, 4), lambda: round_we("vector", 1, 1, 0, 64)],
+            3: [lambda: round_we("vector", 1, 2, 0, 64)],
+            4: [lambda: quantise_we(1, 1, 0, 4)],
+        }
+
+        units = [(0, 0), (0, 1), (1, 0), (1, 1)]
+        h_rows, h_bf, h_codes, h_scales = {}, {}, {}, {}
+
+        def interleave_h(u, n0, n1):
+            nc.vector.tensor_copy(
+                out=h_bf[u][:, 4 * n0 : 4 * n1].rearrange("p (c i t) -> p c t i", i=4, t=4),
+                in_=h_rows[u][:, :, n0:n1].rearrange("p t (c i) -> p c t i", i=4),
+            )
+
+        def quantise_h(u, n0, n1):
+            nc.vector.quantize_mx(
+                out=h_codes[u][:, n0:n1].bitcast(FP8X4),
+                scales=h_scales[u][:, n0:n1],
+                in_=h_bf[u][:, 4 * n0 : 4 * n1],
+            )
+
+        for u, (a, jt) in enumerate(units):
+            h_rows[u] = ring.tile([P, 4, W], BF16, name="h_rows%d" % u, tag="h_rows", align_bytes=64)
+            h_bf[u] = ring.tile([P, 4 * W], BF16, name="h_bf%d" % u, tag="h_bf", align_bytes=64)
+            h_codes[u] = keep.tile([P, W], U32, name="h_codes%d" % u, align_bytes=64)
+            h_scales[u] = keep.tile([P, W], U8, name="h_scales%d" % u, align_bytes=64)
+            for t in range(4):
+                step = 4 * u + t
+                e_ps = bank(t, "e_ps%d" % step)
+                b_ps = bank(4 + t, "b_ps%d" % step)
+                for g in range(2):
+                    nc.tensor.matmul_mx(
+                        out=e_ps[:],
+                        lhsT=we_codes[a, g][:, P * t : P * (t + 1)].bitcast(FP8X4),
+                        lhsT_scale=we_scales[a, g][:, P * t : P * (t + 1)],
+                        rhs=v_codes[jt][:, g, :].bitcast(FP4X4),
+                        rhs_scale=plane_bytes[:, g, V_AT + W * jt : V_AT + W * (jt + 1)],
+                        start=(g == 0),
+                        stop=(g == 1),
+                    )
+                for g in range(2):
+                    c0 = WB_AT + W * a + P * t
+                    nc.tensor.matmul_mx(
+                        out=b_ps[:],
+                        lhsT=wb_codes[a][:, g, 2 * P * t : 2 * P * (t + 1)].bitcast(FP4X4),
+                        lhsT_scale=plane_bytes[:, g, c0 : c0 + P],
+                        rhs=v_codes[jt][:, g, :].bitcast(FP4X4),
+                        rhs_scale=plane_bytes[:, g, V_AT + W * jt : V_AT + W * (jt + 1)],
+                        start=(g == 0),
+                        stop=(g == 1),
+                    )
+                mag = ring.tile([P, W], F32, name="mag%d" % step, tag="mag")
+                logs = ring.tile([P, W], F32, name="logs%d" % step, tag="logs", bufs=6)
+                nc.scalar.activation(out=mag[:], in_=e_ps[:], func=ACT.Abs)
+                pieces = [(0, W // 2), (W // 2, W)] if step == 15 else [(0, W)]
+                for n0, n1 in pieces:
+                    nc.scalar.activation(out=logs[:, n0:n1], in_=mag[:, n0:n1], func=ACT.Ln, bias=1.0)
+                    nc.vector.scalar_tensor_tensor(
+                        out=h_rows[u][:, t, n0:n1],
+                        in0=logs[:, n0:n1],
+                        scalar=gain_sb[:, a, t : t + 1],
+                        in1=b_ps[:, n0:n1],
+                        op0=ALU.mult,
+                        op1=ALU.subtract,
+                    )
+                    if step == 15:
+                        interleave_h(u, n0, n1)
+                if t == 0 and u > 0:
+                    quantise_h(u - 1, 0, W)
+                for job in later.get(step, []):
+                    job()
+            if u < 3:
+                interleave_h(u, 0, W)
+
+        def score_pass(dst, n, jt, a, n0, n1):
+            u = units.index((a, jt))
+            nc.tensor.matmul_mx(
+                out=dst,
+                lhsT=w2_codes[:, a, P * n : P * (n + 1)].bitcast(FP8X4),
+                lhsT_scale=w2_plane_bytes[:, a, P * n : P * (n + 1)],
+                rhs=h_codes[u][:, n0:n1].bitcast(FP8X4),
+                rhs_scale=h_scales[u][:, n0:n1],
+                start=(a == 0),
+                stop=(a == 1),
+            )
+
+        out_v = out.rearrange("(n p) j -> p n j", p=P)
+        half = W // 2
+        quantise_h(3, 0, half)
+        quantise_h(3, half, W)
+        for n in range(4):
+            o_ps = bank(n, "o_ps%d" % n)
+            for a in range(2):
+                score_pass(o_ps[:], n, 0, a, 0, W)
+            res = keep.tile([P, W], F32, name="res0_%d" % n)
+            nc.scalar.copy(out=res[:], in_=o_ps[:])
+            nc.sync.dma_start(out=out_v[:, n, 0:W], in_=res[:])
+        for pair in range(2):
+            o_ps = bank(4 + pair, "o_pa%d" % pair)
+            for k in range(2):
+                for a in range(2):
+                    score_pass(o_ps[:, half * k : half * (k + 1)], 2 * pair + k, 1, a, 0, half)
+            res = keep.tile([P, 2, half], F32, name="res1_%d" % pair)
+            nc.scalar.copy(out=res[:].rearrange("p k j -> p (k j)"), in_=o_ps[:])
+            nc.sync.dma_start(out=out_v[:, 2 * pair : 2 * pair + 2, W : W + half], in_=res[:])
+        last = [bank(b, "o_pb%d" % b) for b in (6, 0, 7, 1)]
+        for a in range(2):
+            for n in range(4):
+                score_pass(last[n][:, 0:half], n, 1, a, half, W)
+        for n in range(4):
+            res = keep.tile([P, half], F32, name="res2_%d" % n)
+            if n % 2 == 0:
+                nc.vector.tensor_copy(out=res[:], in_=last[n][:, 0:half])
+            else:
+                nc.scalar.copy(out=res[:], in_=last[n][:, 0:half])
+            nc.sync.dma_start(out=out_v[:, n, W + half : 2 * W], in_=res[:])

@@ -45,12 +45,13 @@ def tile_list_barcode_programme_scores_kernel(
         warm = keep.tile([P, 1], F32, name="warm")
         warm_out = keep.tile([P, 1], F32, name="warm_out")
 
+        nc.scalar.dma_start(out=gain_sb[:], in_=gain.rearrange("(a p t) -> p a t", a=2, t=4))
         nc.vector.memset(warm[:], 1.0)
         nc.scalar.activation(out=warm_out[:], in_=warm[:], func=ACT.Ln)
-        nc.vector.memset(wb_rows[32:64, :], 0)
-        nc.vector.memset(wb_rows[64:128, :], 0)
         nc.vector.memset(scale_win[32:64, :], 0)
         nc.vector.memset(scale_win[64:128, :], 0)
+        nc.vector.memset(wb_rows[32:64, :], 0)
+        nc.vector.memset(wb_rows[64:128, :], 0)
         nc.vector.memset(planes[:], 0)
 
         nc.sync.dma_start(
@@ -61,7 +62,7 @@ def tile_list_barcode_programme_scores_kernel(
         nc.sync.dma_start(out=wb_rows[0:ROWS, :], in_=wb_scales.rearrange("g q c -> (g q) c").bitcast(I32))
 
         def load_wb(a):
-            raw = reuse.tile([P, 2, W // 2], I32, name="wb_raw%d" % a, align_bytes=64, offset=20480 + 1024 * a)
+            raw = reuse.tile([P, 2, W // 2], I32, name="wb_raw%d" % a, align_bytes=64, offset=(23552, 36864)[a])
             nc.sync.dma_start(
                 out=raw[:],
                 in_=wb_words[:, :, 2 * W * a : 2 * W * (a + 1)].rearrange("g p b -> p g b").bitcast(I32),
@@ -75,31 +76,31 @@ def tile_list_barcode_programme_scores_kernel(
 
         chunks = [(0, 0, 512), (1, 0, 256), (1, 256, 256)]
 
-        def load_we(a):
-            raws = []
-            for i, (g, c0, cw) in enumerate(chunks):
-                raw = keep.tile([P, 4, cw], F32, name="we_raw%d_%d" % (a, i), tag="we_raw%d" % i)
-                nc.sync.dma_start(
-                    out=raw[:],
-                    in_=we[W * g : W * (g + 1), W * a + c0 : W * a + c0 + cw].rearrange("(p j) c -> p j c", j=4),
-                )
-                raws.append(raw)
-            return raws
+        we_raw = {}
 
-        we_raw = {0: load_we(0)}
-        nc.gpsimd.dma_start(out=gain_sb[:], in_=gain.rearrange("(a p t) -> p a t", a=2, t=4))
+        def load_we(a, i):
+            g, c0, cw = chunks[i]
+            raw = reuse.tile(
+                [P, 4, cw], F32, name="we_raw%d_%d" % (a, i), align_bytes=64, offset=(28672, 20480, 24576)[i]
+            )
+            nc.sync.dma_start(
+                out=raw[:],
+                in_=we[W * g : W * (g + 1), W * a + c0 : W * a + c0 + cw].rearrange("(p j) c -> p j c", j=4),
+            )
+            we_raw[a, i] = raw
 
+        load_we(0, 0)
+
+        picked_scales = reuse.tile([P, S], U8, name="picked_scales", align_bytes=64, offset=16384)
+        nc.vector.tensor_copy(picked_scales[:], scale_win[:].bitcast(U8).indirect(offsets[:]))
         nc.vector.tensor_copy(
             out=rows[:].bitcast(U8)[:, WB_AT:PLANE].rearrange("p (a t m) -> p a t m", a=2, t=4),
             in_=wb_rows[:].bitcast(U8).rearrange("p (a m t) -> p a t m", a=2, t=4),
         )
-        picked_scales = keep.tile([P, S], U8, name="picked_scales", align_bytes=64)
-        nc.vector.tensor_copy(picked_scales[:], scale_win[:].bitcast(U8).indirect(offsets[:]))
         nc.vector.tensor_copy(out=rows[:, 0 : S // 4], in_=picked_scales[:].bitcast(I32))
         for g in range(2):
-            queue = nc.scalar if g == 0 else nc.gpsimd
             for q in range(4):
-                queue.dma_start(
+                nc.scalar.dma_start(
                     out=planes[32 * q : 32 * q + 4, g, :], in_=rows[16 * g + 4 * q : 16 * g + 4 * q + 4, :]
                 )
         plane_bytes = planes[:].bitcast(U8)
@@ -107,7 +108,7 @@ def tile_list_barcode_programme_scores_kernel(
         wb_codes = {}
 
         def permute_wb(a):
-            codes = reuse.tile([P, 2, 2 * W], U8, name="wb_codes%d" % a, align_bytes=64, offset=(24576, 6144)[a])
+            codes = reuse.tile([P, 2, 2 * W], U8, name="wb_codes%d" % a, align_bytes=64, offset=(38912, 6144)[a])
             nc.vector.tensor_copy(
                 out=codes[:].bitcast(U16).rearrange("p g (t m) -> p g t m", t=4),
                 in_=wb_raw[a][:].bitcast(U16).rearrange("p g (m t) -> p g t m", t=4),
@@ -115,11 +116,12 @@ def tile_list_barcode_programme_scores_kernel(
             wb_codes[a] = codes
 
         permute_wb(0)
-        wb_raw[1] = load_wb(1)
+        load_we(0, 1)
+        load_we(0, 2)
 
         v_codes = {}
         for jt in range(2):
-            picked = keep.tile([P, W], U32, name="picked_words%d" % jt, align_bytes=64)
+            picked = reuse.tile([P, W], U32, name="picked_words%d" % jt, align_bytes=64, offset=(36864, 40960)[jt])
             nc.vector.tensor_copy(
                 picked[:], word_win[:].bitcast(U32).indirect(offsets[:, 32 * jt : 32 * (jt + 1)])
             )
@@ -128,12 +130,13 @@ def tile_list_barcode_programme_scores_kernel(
                 out=codes[:].bitcast(U16), in_=picked[:].bitcast(U16).rearrange("p (n g) -> p g n", g=2)
             )
             v_codes[jt] = codes
+        wb_raw[1] = load_wb(1)
 
         we_bf, we_codes, we_scales = {}, {}, {}
         for a in range(2):
             for g in range(2):
-                bf_at = {(0, 0): 17408, (0, 1): 0, (1, 0): 28672, (1, 1): 32768}[a, g]
-                codes_at = {(0, 0): 4096, (0, 1): 36864, (1, 0): 38912, (1, 1): 40960}[a, g]
+                bf_at = {(0, 0): 16384, (0, 1): 0, (1, 0): 43008, (1, 1): 47104}[a, g]
+                codes_at = {(0, 0): 4096, (0, 1): 51200, (1, 0): 53248, (1, 1): 55296}[a, g]
                 we_bf[a, g] = reuse.tile([P, 4 * W], BF16, name="we_bf%d%d" % (a, g), align_bytes=64, offset=bf_at)
                 we_codes[a, g] = reuse.tile([P, W], U32, name="we_codes%d%d" % (a, g), align_bytes=64, offset=codes_at)
                 we_scales[a, g] = keep.tile([P, W], U8, name="we_scales%d%d" % (a, g), align_bytes=64)
@@ -141,7 +144,7 @@ def tile_list_barcode_programme_scores_kernel(
         def round_we(engine, a, i, m0, m1):
             g, c0 = chunks[i][0], chunks[i][1]
             dst = we_bf[a, g][:].rearrange("p (t m j) -> p m j t", t=4, j=4)[:, c0 // 4 + m0 : c0 // 4 + m1]
-            src = we_raw[a][i][:].rearrange("p j (m t) -> p m j t", t=4)[:, m0:m1]
+            src = we_raw[a, i][:].rearrange("p j (m t) -> p m j t", t=4)[:, m0:m1]
             if engine == "scalar":
                 nc.scalar.copy(out=dst, in_=src)
             else:
@@ -162,10 +165,11 @@ def tile_list_barcode_programme_scores_kernel(
         for t in range(4):
             quantise_we(0, 1, t, t + 1)
         permute_wb(1)
-        we_raw[1] = load_we(1)
+        for i in range(3):
+            load_we(1, i)
         w2_codes = reuse.tile([P, 2, N], I32, name="w2_codes", align_bytes=64, offset=0)
         nc.sync.dma_start(out=w2_codes[:], in_=w2_words.rearrange("a p c i -> p a (c i)").bitcast(I32))
-        w2_planes = reuse.tile([P, 2, N // 4], I32, name="w2_planes", align_bytes=64, offset=17408)
+        w2_planes = reuse.tile([P, 2, N // 4], I32, name="w2_planes", align_bytes=64, offset=16384)
         nc.vector.memset(w2_planes[:], 0)
         for q in range(4):
             nc.sync.dma_start(
@@ -196,6 +200,21 @@ def tile_list_barcode_programme_scores_kernel(
                 out=h_codes[u][:, n0:n1].bitcast(FP8X4),
                 scales=h_scales[u][:, n0:n1],
                 in_=h_bf[u][:, 4 * n0 : 4 * n1],
+            )
+
+        held = {}
+
+        def correct(step, n0, n1):
+            u, t = divmod(step, 4)
+            mag, logs, b_ps = held[step]
+            nc.scalar.activation(out=logs[:, n0:n1], in_=mag[:, n0:n1], func=ACT.Ln, bias=1.0)
+            nc.vector.scalar_tensor_tensor(
+                out=h_rows[u][:, t, n0:n1],
+                in0=logs[:, n0:n1],
+                scalar=gain_sb[:, units[u][0], t : t + 1],
+                in1=b_ps[:, n0:n1],
+                op0=ALU.mult,
+                op1=ALU.subtract,
             )
 
         for u, (a, jt) in enumerate(units):
@@ -231,19 +250,17 @@ def tile_list_barcode_programme_scores_kernel(
                 mag = ring.tile([P, W], F32, name="mag%d" % step, tag="mag")
                 logs = ring.tile([P, W], F32, name="logs%d" % step, tag="logs", bufs=6)
                 nc.scalar.activation(out=mag[:], in_=e_ps[:], func=ACT.Abs)
-                pieces = [(0, W // 2), (W // 2, W)] if step == 15 else [(0, W)]
-                for n0, n1 in pieces:
-                    nc.scalar.activation(out=logs[:, n0:n1], in_=mag[:, n0:n1], func=ACT.Ln, bias=1.0)
-                    nc.vector.scalar_tensor_tensor(
-                        out=h_rows[u][:, t, n0:n1],
-                        in0=logs[:, n0:n1],
-                        scalar=gain_sb[:, a, t : t + 1],
-                        in1=b_ps[:, n0:n1],
-                        op0=ALU.mult,
-                        op1=ALU.subtract,
-                    )
-                    if step == 15:
-                        interleave_h(u, n0, n1)
+                held[step] = (mag, logs, b_ps)
+                if step < 14:
+                    correct(step, 0, W)
+                else:
+                    correct(step, 0, W // 2)
+                if step == 15:
+                    interleave_h(u, 0, W // 2)
+                    correct(14, W // 2, W)
+                    correct(15, W // 2, W)
+                    quantise_h(u, 0, W // 2)
+                    interleave_h(u, W // 2, W)
                 if t == 0 and u > 0:
                     quantise_h(u - 1, 0, W)
                 for job in later.get(step, []):
@@ -265,7 +282,6 @@ def tile_list_barcode_programme_scores_kernel(
 
         out_v = out.rearrange("(n p) j -> p n j", p=P)
         half = W // 2
-        quantise_h(3, 0, half)
         quantise_h(3, half, W)
         for n in range(4):
             o_ps = bank(n, "o_ps%d" % n)
@@ -280,7 +296,10 @@ def tile_list_barcode_programme_scores_kernel(
                 for a in range(2):
                     score_pass(o_ps[:, half * k : half * (k + 1)], 2 * pair + k, 1, a, 0, half)
             res = keep.tile([P, 2, half], F32, name="res1_%d" % pair)
-            nc.scalar.copy(out=res[:].rearrange("p k j -> p (k j)"), in_=o_ps[:])
+            if pair == 0:
+                nc.scalar.copy(out=res[:].rearrange("p k j -> p (k j)"), in_=o_ps[:])
+            else:
+                nc.vector.tensor_copy(out=res[:].rearrange("p k j -> p (k j)"), in_=o_ps[:])
             nc.sync.dma_start(out=out_v[:, 2 * pair : 2 * pair + 2, W : W + half], in_=res[:])
         last = [bank(b, "o_pb%d" % b) for b in (6, 0, 7, 1)]
         for a in range(2):

@@ -18,8 +18,10 @@ ALU = mybir.AluOpType
 
 P = 128
 W = 512
+HALF = W // 2
 ROWS = 32
 V_AT, WB_AT, PLANE = 0, S, S + H
+KB = 1024
 
 
 def tile_list_barcode_programme_scores_kernel(
@@ -35,24 +37,26 @@ def tile_list_barcode_programme_scores_kernel(
         def bank(i, name):
             return psum.tile([P, W], F32, name=name, tag="bank%d" % i)
 
+        def placed(shape, dtype, name, at):
+            return reuse.tile(shape, dtype, name=name, align_bytes=64, offset=at)
+
         offsets = keep.tile([P, S // 16], U16, name="offsets")
         scale_win = keep.tile([P, T // 4], I32, name="scale_win", align_bytes=64)
-        word_win = reuse.tile([P, T], I32, name="word_win", align_bytes=64, offset=0)
-        planes = keep.tile([P, 2, PLANE // 4], I32, name="planes", align_bytes=64)
-        rows = keep.tile([P, PLANE // 4], I32, name="rows", align_bytes=64)
+        word_win = keep.tile([P, T], I32, name="word_win", align_bytes=64)
+        planes = [keep.tile([P, PLANE // 4], I32, name="plane%d" % g, align_bytes=64) for g in range(2)]
         wb_rows = keep.tile([P, H // 4], I32, name="wb_rows", align_bytes=64)
         gain_sb = keep.tile([P, 2, 4], F32, name="gain_sb")
-        warm = keep.tile([P, 1], F32, name="warm")
-        warm_out = keep.tile([P, 1], F32, name="warm_out")
+        one = keep.tile([P, 1], F32, name="one")
+        zero = keep.tile([P, 1], F32, name="zero")
 
         nc.scalar.dma_start(out=gain_sb[:], in_=gain.rearrange("(a p t) -> p a t", a=2, t=4))
-        nc.vector.memset(warm[:], 1.0)
-        nc.scalar.activation(out=warm_out[:], in_=warm[:], func=ACT.Ln)
+        nc.vector.memset(one[:], 1.0)
+        nc.scalar.activation(out=zero[:], in_=one[:], func=ACT.Ln)
         nc.vector.memset(scale_win[32:64, :], 0)
         nc.vector.memset(scale_win[64:128, :], 0)
         nc.vector.memset(wb_rows[32:64, :], 0)
         nc.vector.memset(wb_rows[64:128, :], 0)
-        nc.vector.memset(planes[:], 0)
+        nc.vector.memset(planes[1][:], 0)
 
         nc.sync.dma_start(
             out=scale_win[0:ROWS, :],
@@ -61,67 +65,95 @@ def tile_list_barcode_programme_scores_kernel(
         nc.sync.dma_start(offsets[:], offs)
         nc.sync.dma_start(out=wb_rows[0:ROWS, :], in_=wb_scales.rearrange("g q c -> (g q) c").bitcast(I32))
 
-        def load_wb(a):
-            raw = reuse.tile([P, 2, W // 2], I32, name="wb_raw%d" % a, align_bytes=64, offset=(23552, 36864)[a])
+        wb_raw, we_raw = {}, {}
+
+        def load_wb(a, at):
+            held = placed([P, W + (32 if a == 0 else 0)], I32, "wb_raw%d" % a, at)
+            wb_raw[a] = held[:, 0:W].rearrange("p (g b) -> p g b", g=2)
             nc.sync.dma_start(
-                out=raw[:],
+                out=wb_raw[a],
                 in_=wb_words[:, :, 2 * W * a : 2 * W * (a + 1)].rearrange("g p b -> p g b").bitcast(I32),
             )
-            return raw
 
-        wb_raw = {0: load_wb(0)}
-        nc.sync.dma_start(
-            out=word_win[:], in_=tab[0, 0 : 512 * T].rearrange("(p b) -> p b", p=P).bitcast(I32)
-        )
-
-        chunks = [(0, 0, 512), (1, 0, 256), (1, 256, 256)]
-
-        we_raw = {}
-
-        def load_we(a, i):
-            g, c0, cw = chunks[i]
-            raw = reuse.tile(
-                [P, 4, cw], F32, name="we_raw%d_%d" % (a, i), align_bytes=64, offset=(28672, 20480, 24576)[i]
-            )
+        def load_we(a, g, c0, cw, at):
+            raw = placed([P, 4, cw], F32, "we_raw%d%d_%d" % (a, g, c0), at)
             nc.sync.dma_start(
                 out=raw[:],
                 in_=we[W * g : W * (g + 1), W * a + c0 : W * a + c0 + cw].rearrange("(p j) c -> p j c", j=4),
             )
-            we_raw[a, i] = raw
+            we_raw[a, g, c0] = raw
 
-        load_we(0, 0)
+        load_wb(0, 17 * KB - 64)
+        nc.sync.dma_start(
+            out=word_win[:], in_=tab[0, 0 : 512 * T].rearrange("(p b) -> p b", p=P).bitcast(I32)
+        )
+        load_we(0, 0, 0, W, 28 * KB)
 
-        picked_scales = reuse.tile([P, S], U8, name="picked_scales", align_bytes=64, offset=16384)
+        picked_scales = placed([P, S], U8, "picked_scales", 4 * KB - KB // 2)
         nc.vector.tensor_copy(picked_scales[:], scale_win[:].bitcast(U8).indirect(offsets[:]))
         nc.vector.tensor_copy(
-            out=rows[:].bitcast(U8)[:, WB_AT:PLANE].rearrange("p (a t m) -> p a t m", a=2, t=4),
+            out=planes[0][:].bitcast(U8)[:, WB_AT:PLANE].rearrange("p (a t m) -> p a t m", a=2, t=4),
             in_=wb_rows[:].bitcast(U8).rearrange("p (a m t) -> p a t m", a=2, t=4),
         )
-        nc.vector.tensor_copy(out=rows[:, 0 : S // 4], in_=picked_scales[:].bitcast(I32))
+        nc.vector.tensor_copy(out=planes[0][:, 0 : S // 4], in_=picked_scales[:].bitcast(I32))
         for g in range(2):
             for q in range(4):
-                nc.scalar.dma_start(
-                    out=planes[32 * q : 32 * q + 4, g, :], in_=rows[16 * g + 4 * q : 16 * g + 4 * q + 4, :]
-                )
-        plane_bytes = planes[:].bitcast(U8)
+                if (g, q) == (1, 3):
+                    load_we(0, 1, 0, HALF, 0)
+                if (g, q) != (0, 0):
+                    nc.sync.dma_start(
+                        out=planes[g][32 * q : 32 * q + 4, :], in_=planes[0][16 * g + 4 * q : 16 * g + 4 * q + 4, :]
+                    )
+        load_we(0, 1, HALF, HALF, 4 * KB)
+        plane_bytes = [pl[:].bitcast(U8) for pl in planes]
 
         wb_codes = {}
 
-        def permute_wb(a):
-            codes = reuse.tile([P, 2, 2 * W], U8, name="wb_codes%d" % a, align_bytes=64, offset=(38912, 6144)[a])
+        def permute_wb(a, at):
+            wb_codes[a] = placed([P, 2, 2 * W], U8, "wb_codes%d" % a, at)
             nc.vector.tensor_copy(
-                out=codes[:].bitcast(U16).rearrange("p g (t m) -> p g t m", t=4),
-                in_=wb_raw[a][:].bitcast(U16).rearrange("p g (m t) -> p g t m", t=4),
+                out=wb_codes[a][:].bitcast(U16).rearrange("p g (t m) -> p g t m", t=4),
+                in_=wb_raw[a].bitcast(U16).rearrange("p g (m t) -> p g t m", t=4),
             )
-            wb_codes[a] = codes
 
-        permute_wb(0)
-        load_we(0, 1)
-        load_we(0, 2)
+        permute_wb(0, 36 * KB)
+        load_wb(1, 17 * KB)
+        load_we(1, 0, 0, W, 9 * KB)
+        load_we(1, 1, 0, W, 19 * KB)
+
+        LOGS_AT = 48 * KB
+        we_bf, we_codes, we_scales = {}, {}, {}
+        bf_at = {(0, 0): 94 * KB, (0, 1): 88 * KB, (1, 0): LOGS_AT - 0 * KB + 32 * KB, (1, 1): LOGS_AT + 36 * KB}
+        logs_at = [LOGS_AT + 2 * KB * s for s in range(16)]
+        logs_at[0] = bf_at[1, 0]
+        logs_at[2] = bf_at[1, 1]
+
+        def round_we(engine, a, g, c0, m0, m1):
+            if (a, g) not in we_bf:
+                we_bf[a, g] = placed([P, 4 * W], BF16, "we_bf%d%d" % (a, g), bf_at[a, g])
+            dst = we_bf[a, g][:].rearrange("p (t m j) -> p m t j", t=4, j=4)[:, c0 // 4 + m0 : c0 // 4 + m1]
+            src = we_raw[a, g, c0][:].rearrange("p j (m t) -> p m t j", t=4)[:, m0:m1]
+            if engine == "scalar":
+                nc.scalar.copy(out=dst, in_=src)
+            else:
+                nc.vector.tensor_copy(out=dst, in_=src)
+
+        def quantise_we(a, g, t0, t1, at=None):
+            name = "%d%d%d" % (a, g, t0)
+            width = P * (t1 - t0)
+            if at is None:
+                codes = keep.tile([P, width], U32, name="we_codes" + name, align_bytes=64)
+            else:
+                codes = placed([P, width], U32, "we_codes" + name, at)
+            scales = keep.tile([P, width], U8, name="we_scales" + name, align_bytes=64)
+            nc.vector.quantize_mx(out=codes[:].bitcast(FP8X4), scales=scales[:], in_=we_bf[a, g][:, W * t0 : W * t1])
+            for t in range(t0, t1):
+                we_codes[a, g, t] = codes[:, P * (t - t0) : P * (t - t0 + 1)]
+                we_scales[a, g, t] = scales[:, P * (t - t0) : P * (t - t0 + 1)]
 
         v_codes = {}
         for jt in range(2):
-            picked = reuse.tile([P, W], U32, name="picked_words%d" % jt, align_bytes=64, offset=(36864, 40960)[jt])
+            picked = placed([P, W], U32, "picked_words%d" % jt, (92 - jt) * KB)
             nc.vector.tensor_copy(
                 picked[:], word_win[:].bitcast(U32).indirect(offsets[:, 32 * jt : 32 * (jt + 1)])
             )
@@ -130,46 +162,20 @@ def tile_list_barcode_programme_scores_kernel(
                 out=codes[:].bitcast(U16), in_=picked[:].bitcast(U16).rearrange("p (n g) -> p g n", g=2)
             )
             v_codes[jt] = codes
-        wb_raw[1] = load_wb(1)
 
-        we_bf, we_codes, we_scales = {}, {}, {}
-        for a in range(2):
-            for g in range(2):
-                bf_at = {(0, 0): 16384, (0, 1): 0, (1, 0): 43008, (1, 1): 47104}[a, g]
-                codes_at = {(0, 0): 4096, (0, 1): 51200, (1, 0): 53248, (1, 1): 55296}[a, g]
-                we_bf[a, g] = reuse.tile([P, 4 * W], BF16, name="we_bf%d%d" % (a, g), align_bytes=64, offset=bf_at)
-                we_codes[a, g] = reuse.tile([P, W], U32, name="we_codes%d%d" % (a, g), align_bytes=64, offset=codes_at)
-                we_scales[a, g] = keep.tile([P, W], U8, name="we_scales%d%d" % (a, g), align_bytes=64)
+        round_we("scalar", 0, 0, 0, 0, 128)
+        quantise_we(0, 0, 0, 2)
+        round_we("scalar", 0, 1, 0, 0, 64)
+        round_we("vector", 0, 1, HALF, 0, 64)
+        quantise_we(0, 1, 0, 1)
+        quantise_we(0, 1, 1, 2)
+        quantise_we(0, 1, 2, 4)
+        quantise_we(0, 0, 2, 4, 90 * KB)
+        permute_wb(1, 88 * KB)
 
-        def round_we(engine, a, i, m0, m1):
-            g, c0 = chunks[i][0], chunks[i][1]
-            dst = we_bf[a, g][:].rearrange("p (t m j) -> p m j t", t=4, j=4)[:, c0 // 4 + m0 : c0 // 4 + m1]
-            src = we_raw[a, i][:].rearrange("p j (m t) -> p m j t", t=4)[:, m0:m1]
-            if engine == "scalar":
-                nc.scalar.copy(out=dst, in_=src)
-            else:
-                nc.vector.tensor_copy(out=dst, in_=src)
-
-        def quantise_we(a, g, t0, t1):
-            nc.vector.quantize_mx(
-                out=we_codes[a, g][:, P * t0 : P * t1].bitcast(FP8X4),
-                scales=we_scales[a, g][:, P * t0 : P * t1],
-                in_=we_bf[a, g][:, W * t0 : W * t1],
-            )
-
-        round_we("scalar", 0, 0, 0, 128)
-        quantise_we(0, 0, 0, 4)
-        round_we("vector", 0, 1, 0, 64)
-        round_we("vector", 0, 2, 0, 40)
-        round_we("scalar", 0, 2, 40, 64)
-        for t in range(4):
-            quantise_we(0, 1, t, t + 1)
-        permute_wb(1)
-        for i in range(3):
-            load_we(1, i)
-        w2_codes = reuse.tile([P, 2, N], I32, name="w2_codes", align_bytes=64, offset=0)
+        w2_codes = placed([P, 2, N], I32, "w2_codes", 0)
         nc.sync.dma_start(out=w2_codes[:], in_=w2_words.rearrange("a p c i -> p a (c i)").bitcast(I32))
-        w2_planes = reuse.tile([P, 2, N // 4], I32, name="w2_planes", align_bytes=64, offset=16384)
+        w2_planes = placed([P, 2, N // 4], I32, "w2_planes", 4 * KB)
         nc.vector.memset(w2_planes[:], 0)
         for q in range(4):
             nc.sync.dma_start(
@@ -178,95 +184,77 @@ def tile_list_barcode_programme_scores_kernel(
             )
         w2_plane_bytes = w2_planes[:].bitcast(U8)
 
-        later = {
-            0: [lambda: round_we("vector", 1, 0, 0, 64)],
-            1: [lambda: round_we("vector", 1, 0, 64, 128)],
-            2: [lambda: quantise_we(1, 0, 0, 4), lambda: round_we("vector", 1, 1, 0, 64)],
-            3: [lambda: round_we("vector", 1, 2, 0, 64)],
-            4: [lambda: quantise_we(1, 1, 0, 4)],
-        }
-
         units = [(0, 0), (0, 1), (1, 0), (1, 1)]
         h_rows, h_bf, h_codes, h_scales = {}, {}, {}, {}
+        e_ps, b_ps, mags, logs = {}, {}, {}, {}
+
+        def e_pass(step, g):
+            (a, jt), t = units[step // 4], step % 4
+            if g == 0:
+                e_ps[step] = bank(t, "e_ps%d" % step)
+            nc.tensor.matmul_mx(
+                out=e_ps[step][:],
+                lhsT=we_codes[a, g, t].bitcast(FP8X4),
+                lhsT_scale=we_scales[a, g, t],
+                rhs=v_codes[jt][:, g, :].bitcast(FP4X4),
+                rhs_scale=plane_bytes[g][:, V_AT + W * jt : V_AT + W * (jt + 1)],
+                start=(g == 0),
+                stop=(g == 1),
+            )
+
+        def b_pass(step, g):
+            (a, jt), t = units[step // 4], step % 4
+            if g == 0:
+                b_ps[step] = bank(4 + t, "b_ps%d" % step)
+            c0 = WB_AT + W * a + P * t
+            nc.tensor.matmul_mx(
+                out=b_ps[step][:],
+                lhsT=wb_codes[a][:, g, 2 * P * t : 2 * P * (t + 1)].bitcast(FP4X4),
+                lhsT_scale=plane_bytes[g][:, c0 : c0 + P],
+                rhs=v_codes[jt][:, g, :].bitcast(FP4X4),
+                rhs_scale=plane_bytes[g][:, V_AT + W * jt : V_AT + W * (jt + 1)],
+                start=(g == 0),
+                stop=(g == 1),
+            )
+
+        def magnitude(step):
+            mags[step] = ring.tile([P, W], F32, name="mag%d" % step, tag="mag", bufs=3)
+            nc.scalar.activation(out=mags[step][:], in_=e_ps[step][:], func=ACT.Abs, bias=zero[:])
+
+        def logarithm(step):
+            logs[step] = placed([P, W], F32, "logs%d" % step, logs_at[step])
+            nc.scalar.activation(out=logs[step][:], in_=mags[step][:], func=ACT.Ln, bias=1.0)
+
+        def correct(step, n0, n1):
+            u, t = divmod(step, 4)
+            if u not in h_rows:
+                h_rows[u] = ring.tile([P, 4, W], BF16, name="h_rows%d" % u, tag="h_rows", align_bytes=64, bufs=3)
+            nc.vector.scalar_tensor_tensor(
+                out=h_rows[u][:, t, n0:n1],
+                in0=logs[step][:, n0:n1],
+                scalar=gain_sb[:, units[u][0], t : t + 1],
+                in1=b_ps[step][:, n0:n1],
+                op0=ALU.mult,
+                op1=ALU.subtract,
+            )
 
         def interleave_h(u, n0, n1):
+            if u not in h_bf:
+                h_bf[u] = ring.tile([P, 4 * W], BF16, name="h_bf%d" % u, tag="h_bf", align_bytes=64)
             nc.vector.tensor_copy(
                 out=h_bf[u][:, 4 * n0 : 4 * n1].rearrange("p (c i t) -> p c t i", i=4, t=4),
                 in_=h_rows[u][:, :, n0:n1].rearrange("p t (c i) -> p c t i", i=4),
             )
 
         def quantise_h(u, n0, n1):
+            if u not in h_codes:
+                h_codes[u] = keep.tile([P, W], U32, name="h_codes%d" % u, align_bytes=64)
+                h_scales[u] = keep.tile([P, W], U8, name="h_scales%d" % u, align_bytes=64)
             nc.vector.quantize_mx(
                 out=h_codes[u][:, n0:n1].bitcast(FP8X4),
                 scales=h_scales[u][:, n0:n1],
                 in_=h_bf[u][:, 4 * n0 : 4 * n1],
             )
-
-        held = {}
-
-        def correct(step, n0, n1):
-            u, t = divmod(step, 4)
-            mag, logs, b_ps = held[step]
-            nc.scalar.activation(out=logs[:, n0:n1], in_=mag[:, n0:n1], func=ACT.Ln, bias=1.0)
-            nc.vector.scalar_tensor_tensor(
-                out=h_rows[u][:, t, n0:n1],
-                in0=logs[:, n0:n1],
-                scalar=gain_sb[:, units[u][0], t : t + 1],
-                in1=b_ps[:, n0:n1],
-                op0=ALU.mult,
-                op1=ALU.subtract,
-            )
-
-        for u, (a, jt) in enumerate(units):
-            h_rows[u] = ring.tile([P, 4, W], BF16, name="h_rows%d" % u, tag="h_rows", align_bytes=64)
-            h_bf[u] = ring.tile([P, 4 * W], BF16, name="h_bf%d" % u, tag="h_bf", align_bytes=64)
-            h_codes[u] = keep.tile([P, W], U32, name="h_codes%d" % u, align_bytes=64)
-            h_scales[u] = keep.tile([P, W], U8, name="h_scales%d" % u, align_bytes=64)
-            for t in range(4):
-                step = 4 * u + t
-                e_ps = bank(t, "e_ps%d" % step)
-                b_ps = bank(4 + t, "b_ps%d" % step)
-                for g in range(2):
-                    nc.tensor.matmul_mx(
-                        out=e_ps[:],
-                        lhsT=we_codes[a, g][:, P * t : P * (t + 1)].bitcast(FP8X4),
-                        lhsT_scale=we_scales[a, g][:, P * t : P * (t + 1)],
-                        rhs=v_codes[jt][:, g, :].bitcast(FP4X4),
-                        rhs_scale=plane_bytes[:, g, V_AT + W * jt : V_AT + W * (jt + 1)],
-                        start=(g == 0),
-                        stop=(g == 1),
-                    )
-                for g in range(2):
-                    c0 = WB_AT + W * a + P * t
-                    nc.tensor.matmul_mx(
-                        out=b_ps[:],
-                        lhsT=wb_codes[a][:, g, 2 * P * t : 2 * P * (t + 1)].bitcast(FP4X4),
-                        lhsT_scale=plane_bytes[:, g, c0 : c0 + P],
-                        rhs=v_codes[jt][:, g, :].bitcast(FP4X4),
-                        rhs_scale=plane_bytes[:, g, V_AT + W * jt : V_AT + W * (jt + 1)],
-                        start=(g == 0),
-                        stop=(g == 1),
-                    )
-                mag = ring.tile([P, W], F32, name="mag%d" % step, tag="mag")
-                logs = ring.tile([P, W], F32, name="logs%d" % step, tag="logs", bufs=6)
-                nc.scalar.activation(out=mag[:], in_=e_ps[:], func=ACT.Abs)
-                held[step] = (mag, logs, b_ps)
-                if step < 14:
-                    correct(step, 0, W)
-                else:
-                    correct(step, 0, W // 2)
-                if step == 15:
-                    interleave_h(u, 0, W // 2)
-                    correct(14, W // 2, W)
-                    correct(15, W // 2, W)
-                    quantise_h(u, 0, W // 2)
-                    interleave_h(u, W // 2, W)
-                if t == 0 and u > 0:
-                    quantise_h(u - 1, 0, W)
-                for job in later.get(step, []):
-                    job()
-            if u < 3:
-                interleave_h(u, 0, W)
 
         def score_pass(dst, n, jt, a, n0, n1):
             u = units.index((a, jt))
@@ -280,9 +268,54 @@ def tile_list_barcode_programme_scores_kernel(
                 stop=(a == 1),
             )
 
+        later = {
+            0: [lambda: round_we("vector", 1, 0, 0, 0, 128)],
+            1: [lambda: quantise_we(1, 0, 0, 4)],
+            2: [lambda: round_we("vector", 1, 1, 0, 0, 128)],
+            3: [lambda: quantise_we(1, 1, 0, 4)],
+            5: [lambda: interleave_h(0, 0, W)],
+            6: [lambda: quantise_h(0, 0, W)],
+            8: [lambda: interleave_h(1, 0, W)],
+            9: [lambda: quantise_h(1, 0, W)],
+        }
+
+        for g in range(2):
+            for t in range(4):
+                b_pass(t, g)
+        e_pass(0, 0)
+        e_pass(1, 0)
+        e_pass(0, 1)
+        magnitude(0)
+        for step in range(16):
+            if step < 15:
+                if step + 1 >= 2:
+                    e_pass(step + 1, 0)
+                e_pass(step + 1, 1)
+                magnitude(step + 1)
+            if step >= 4:
+                b_pass(step, 0)
+                b_pass(step, 1)
+            logarithm(step)
+            if step < 12:
+                correct(step, 0, W)
+            else:
+                correct(step, 0, HALF)
+            if step == 12:
+                interleave_h(2, 0, W)
+            if step == 13:
+                quantise_h(2, 0, W)
+            for job in later.get(step, []):
+                job()
+
         out_v = out.rearrange("(n p) j -> p n j", p=P)
-        half = W // 2
-        quantise_h(3, half, W)
+        correct(12, HALF, W)
+        interleave_h(3, 0, HALF)
+        correct(13, HALF, W)
+        quantise_h(3, 0, HALF)
+        correct(14, HALF, W)
+        correct(15, HALF, W)
+        interleave_h(3, HALF, W)
+        quantise_h(3, HALF, W)
         for n in range(4):
             o_ps = bank(n, "o_ps%d" % n)
             for a in range(2):
@@ -291,24 +324,21 @@ def tile_list_barcode_programme_scores_kernel(
             nc.scalar.copy(out=res[:], in_=o_ps[:])
             nc.sync.dma_start(out=out_v[:, n, 0:W], in_=res[:])
         for pair in range(2):
-            o_ps = bank(4 + pair, "o_pa%d" % pair)
+            o_ps = bank(pair, "o_pa%d" % pair)
             for k in range(2):
                 for a in range(2):
-                    score_pass(o_ps[:, half * k : half * (k + 1)], 2 * pair + k, 1, a, 0, half)
-            res = keep.tile([P, 2, half], F32, name="res1_%d" % pair)
-            if pair == 0:
-                nc.scalar.copy(out=res[:].rearrange("p k j -> p (k j)"), in_=o_ps[:])
-            else:
-                nc.vector.tensor_copy(out=res[:].rearrange("p k j -> p (k j)"), in_=o_ps[:])
-            nc.sync.dma_start(out=out_v[:, 2 * pair : 2 * pair + 2, W : W + half], in_=res[:])
-        last = [bank(b, "o_pb%d" % b) for b in (6, 0, 7, 1)]
+                    score_pass(o_ps[:, HALF * k : HALF * (k + 1)], 2 * pair + k, 1, a, 0, HALF)
+            res = keep.tile([P, 2, HALF], F32, name="res1_%d" % pair)
+            nc.scalar.copy(out=res[:].rearrange("p k j -> p (k j)"), in_=o_ps[:])
+            nc.sync.dma_start(out=out_v[:, 2 * pair : 2 * pair + 2, W : W + HALF], in_=res[:])
+        last = [bank(4 + n, "o_pb%d" % n) for n in range(4)]
         for a in range(2):
             for n in range(4):
-                score_pass(last[n][:, 0:half], n, 1, a, half, W)
+                score_pass(last[n][:, 0:HALF], n, 1, a, HALF, W)
         for n in range(4):
-            res = keep.tile([P, half], F32, name="res2_%d" % n)
+            res = keep.tile([P, HALF], F32, name="res2_%d" % n)
             if n % 2 == 0:
-                nc.vector.tensor_copy(out=res[:], in_=last[n][:, 0:half])
+                nc.vector.tensor_copy(out=res[:], in_=last[n][:, 0:HALF])
             else:
-                nc.scalar.copy(out=res[:], in_=last[n][:, 0:half])
-            nc.sync.dma_start(out=out_v[:, n, W + half : 2 * W], in_=res[:])
+                nc.scalar.copy(out=res[:], in_=last[n][:, 0:HALF])
+            nc.sync.dma_start(out=out_v[:, n, W + HALF : 2 * W], in_=res[:])

@@ -123,10 +123,9 @@ def tile_list_barcode_programme_scores_kernel(
 
         LOGS_AT = 48 * KB
         we_bf, we_codes, we_scales = {}, {}, {}
-        bf_at = {(0, 0): 94 * KB, (0, 1): 88 * KB, (1, 0): LOGS_AT - 0 * KB + 32 * KB, (1, 1): LOGS_AT + 36 * KB}
-        logs_at = [LOGS_AT + 2 * KB * s for s in range(16)]
-        logs_at[0] = bf_at[1, 0]
-        logs_at[2] = bf_at[1, 1]
+        bf_at = {(0, 0): 93 * KB, (0, 1): 88 * KB, (1, 0): 93 * KB, (1, 1): LOGS_AT + 36 * KB}
+        logs_at = [LOGS_AT + 4 * KB * s for s in range(8)]
+        logs_at[0] = bf_at[1, 1]
 
         def round_we(engine, a, g, c0, m0, m1):
             if (a, g) not in we_bf:
@@ -163,7 +162,8 @@ def tile_list_barcode_programme_scores_kernel(
             )
             v_codes[jt] = codes
 
-        round_we("scalar", 0, 0, 0, 0, 128)
+        round_we("scalar", 0, 0, 0, 0, 96)
+        round_we("vector", 0, 0, 0, 96, 128)
         quantise_we(0, 0, 0, 2)
         round_we("scalar", 0, 1, 0, 0, 64)
         round_we("vector", 0, 1, HALF, 0, 64)
@@ -218,12 +218,14 @@ def tile_list_barcode_programme_scores_kernel(
             )
 
         def magnitude(step):
-            mags[step] = ring.tile([P, W], F32, name="mag%d" % step, tag="mag", bufs=3)
-            nc.scalar.activation(out=mags[step][:], in_=e_ps[step][:], func=ACT.Abs, bias=zero[:])
+            if step % 2 == 0:
+                mags[step // 2] = ring.tile([P, 2, W], F32, name="mag%d" % step, tag="mag", bufs=3)
+            nc.scalar.activation(out=mags[step // 2][:, step % 2, :], in_=e_ps[step][:], func=ACT.Abs, bias=zero[:])
 
-        def logarithm(step):
-            logs[step] = placed([P, W], F32, "logs%d" % step, logs_at[step])
-            nc.scalar.activation(out=logs[step][:], in_=mags[step][:], func=ACT.Ln, bias=1.0)
+        def logarithm(pair, n0, n1, k0=0, k1=2):
+            if pair not in logs:
+                logs[pair] = placed([P, 2, W], F32, "logs%d" % pair, logs_at[pair])
+            nc.scalar.activation(out=logs[pair][:, k0:k1, n0:n1], in_=mags[pair][:, k0:k1, n0:n1], func=ACT.Ln, bias=1.0)
 
         def correct(step, n0, n1):
             u, t = divmod(step, 4)
@@ -231,7 +233,7 @@ def tile_list_barcode_programme_scores_kernel(
                 h_rows[u] = ring.tile([P, 4, W], BF16, name="h_rows%d" % u, tag="h_rows", align_bytes=64, bufs=3)
             nc.vector.scalar_tensor_tensor(
                 out=h_rows[u][:, t, n0:n1],
-                in0=logs[step][:, n0:n1],
+                in0=logs[step // 2][:, step % 2, n0:n1],
                 scalar=gain_sb[:, units[u][0], t : t + 1],
                 in1=b_ps[step][:, n0:n1],
                 op0=ALU.mult,
@@ -239,6 +241,17 @@ def tile_list_barcode_programme_scores_kernel(
             )
 
         def interleave_h(u, n0, n1):
+            if u < 2:
+                h_bf[u] = placed([P, 4 * W], BF16, "h_bf%d" % u, bf_at[1, 1])
+                nc.gpsimd.tensor_scalar(
+                    out=h_bf[u][:].rearrange("p (n t) -> p n t", t=4),
+                    in0=h_rows[u][:].rearrange("p t n -> p n t"),
+                    scalar1=1.0,
+                    scalar2=0.0,
+                    op0=ALU.mult,
+                    op1=ALU.add,
+                )
+                return
             if u not in h_bf:
                 h_bf[u] = ring.tile([P, 4 * W], BF16, name="h_bf%d" % u, tag="h_bf", align_bytes=64)
             nc.vector.tensor_copy(
@@ -256,7 +269,7 @@ def tile_list_barcode_programme_scores_kernel(
                 in_=h_bf[u][:, 4 * n0 : 4 * n1],
             )
 
-        def score_pass(dst, n, jt, a, n0, n1):
+        def score_pass(dst, n, jt, a, n0, n1, start, stop):
             u = units.index((a, jt))
             nc.tensor.matmul_mx(
                 out=dst,
@@ -264,81 +277,89 @@ def tile_list_barcode_programme_scores_kernel(
                 lhsT_scale=w2_plane_bytes[:, a, P * n : P * (n + 1)],
                 rhs=h_codes[u][:, n0:n1].bitcast(FP8X4),
                 rhs_scale=h_scales[u][:, n0:n1],
-                start=(a == 0),
-                stop=(a == 1),
+                start=start,
+                stop=stop,
             )
 
         later = {
-            0: [lambda: round_we("vector", 1, 0, 0, 0, 128)],
-            1: [lambda: quantise_we(1, 0, 0, 4)],
-            2: [lambda: round_we("vector", 1, 1, 0, 0, 128)],
-            3: [lambda: quantise_we(1, 1, 0, 4)],
-            5: [lambda: interleave_h(0, 0, W)],
+            0: [lambda: quantise_we(1, 0, 0, 4)],
+            1: [lambda: round_we("vector", 1, 1, 0, 0, 128)],
+            2: [lambda: quantise_we(1, 1, 0, 4)],
+            11: [lambda: interleave_h(2, 0, W), lambda: quantise_h(2, 0, W)],
+            3: [lambda: interleave_h(0, 0, W)],
             6: [lambda: quantise_h(0, 0, W)],
-            8: [lambda: interleave_h(1, 0, W)],
-            9: [lambda: quantise_h(1, 0, W)],
+            7: [lambda: interleave_h(1, 0, W)],
+            10: [lambda: quantise_h(1, 0, W)],
         }
 
         for g in range(2):
             for t in range(4):
                 b_pass(t, g)
+        def products(step):
+            if step >= 2:
+                e_pass(step, 0)
+            e_pass(step, 1)
+            magnitude(step)
+            if step >= 5:
+                b_pass(step - 1, 0)
+                b_pass(step - 1, 1)
+
+        round_we("vector", 1, 0, 0, 0, 128)
         e_pass(0, 0)
         e_pass(1, 0)
-        e_pass(0, 1)
-        magnitude(0)
-        for step in range(16):
-            if step < 15:
-                if step + 1 >= 2:
-                    e_pass(step + 1, 0)
-                e_pass(step + 1, 1)
-                magnitude(step + 1)
-            if step >= 4:
-                b_pass(step, 0)
-                b_pass(step, 1)
-            logarithm(step)
-            if step < 12:
-                correct(step, 0, W)
+        products(0)
+        products(1)
+        for pair in range(6):
+            if pair < 5:
+                products(2 * pair + 2)
+                logarithm(pair, 0, W)
             else:
-                correct(step, 0, HALF)
-            if step == 12:
-                interleave_h(2, 0, W)
-            if step == 13:
-                quantise_h(2, 0, W)
-            for job in later.get(step, []):
-                job()
-
-        out_v = out.rearrange("(n p) j -> p n j", p=P)
-        correct(12, HALF, W)
+                logarithm(pair, 0, W, 0, 1)
+                logarithm(pair, 0, W, 1, 2)
+                products(2 * pair + 2)
+            for step in (2 * pair, 2 * pair + 1):
+                correct(step, 0, W)
+                for job in later.get(step, []):
+                    job()
+            products(2 * pair + 3)
+        products(14)
+        logarithm(6, 0, W)
+        correct(12, 0, W)
+        correct(13, 0, W)
+        products(15)
+        b_pass(15, 0)
+        b_pass(15, 1)
+        logarithm(7, 0, HALF)
+        logarithm(7, HALF, W)
+        correct(14, 0, HALF)
+        correct(15, 0, HALF)
         interleave_h(3, 0, HALF)
-        correct(13, HALF, W)
-        quantise_h(3, 0, HALF)
         correct(14, HALF, W)
         correct(15, HALF, W)
+        quantise_h(3, 0, HALF)
         interleave_h(3, HALF, W)
         quantise_h(3, HALF, W)
-        for n in range(4):
-            o_ps = bank(n, "o_ps%d" % n)
-            for a in range(2):
-                score_pass(o_ps[:], n, 0, a, 0, W)
-            res = keep.tile([P, W], F32, name="res0_%d" % n)
-            nc.scalar.copy(out=res[:], in_=o_ps[:])
-            nc.sync.dma_start(out=out_v[:, n, 0:W], in_=res[:])
-        for pair in range(2):
-            o_ps = bank(pair, "o_pa%d" % pair)
-            for k in range(2):
-                for a in range(2):
-                    score_pass(o_ps[:, HALF * k : HALF * (k + 1)], 2 * pair + k, 1, a, 0, HALF)
-            res = keep.tile([P, 2, HALF], F32, name="res1_%d" % pair)
-            nc.scalar.copy(out=res[:].rearrange("p k j -> p (k j)"), in_=o_ps[:])
-            nc.sync.dma_start(out=out_v[:, 2 * pair : 2 * pair + 2, W : W + HALF], in_=res[:])
-        last = [bank(4 + n, "o_pb%d" % n) for n in range(4)]
+
+        out_v = out.rearrange("(n p) j -> p n j", p=P)
+        first = [bank(n, "o_ps%d" % n) for n in range(4)]
         for a in range(2):
             for n in range(4):
-                score_pass(last[n][:, 0:HALF], n, 1, a, HALF, W)
+                score_pass(first[n][:], n, 0, a, 0, W, a == 0, a == 1)
         for n in range(4):
-            res = keep.tile([P, HALF], F32, name="res2_%d" % n)
-            if n % 2 == 0:
-                nc.vector.tensor_copy(out=res[:], in_=last[n][:, 0:HALF])
-            else:
-                nc.scalar.copy(out=res[:], in_=last[n][:, 0:HALF])
-            nc.sync.dma_start(out=out_v[:, n, W + HALF : 2 * W], in_=res[:])
+            res = keep.tile([P, W], F32, name="res0_%d" % n)
+            nc.scalar.copy(out=res[:], in_=first[n][:])
+            nc.sync.dma_start(out=out_v[:, n, 0:W], in_=res[:])
+        for half in range(2):
+            pairs = [bank(4 + 2 * half + pair, "o_ps%d%d" % (half, pair)) for pair in range(2)]
+            for a in range(2):
+                for n in range(4):
+                    dst = pairs[n // 2][:, HALF * (n % 2) : HALF * (n % 2 + 1)]
+                    score_pass(dst, n, 1, a, HALF * half, HALF * (half + 1), (a, n % 2) == (0, 0), (a, n % 2) == (1, 1))
+            for pair in range(2):
+                res = keep.tile([P, 2, HALF], F32, name="res1_%d%d" % (half, pair))
+                if pair == 0:
+                    nc.vector.tensor_copy(out=res[:].rearrange("p k j -> p (k j)"), in_=pairs[pair][:])
+                else:
+                    nc.scalar.copy(out=res[:].rearrange("p k j -> p (k j)"), in_=pairs[pair][:])
+                c0 = W + HALF * half
+                nc.sync.dma_start(out=out_v[:, 2 * pair : 2 * pair + 2, c0 : c0 + HALF], in_=res[:])

@@ -254,6 +254,16 @@ def tile_list_barcode_programme_scores_kernel(
                 return
             if u not in h_bf:
                 h_bf[u] = ring.tile([P, 4 * W], BF16, name="h_bf%d" % u, tag="h_bf", align_bytes=64)
+            if (u, n0) == (3, 0):
+                nc.gpsimd.tensor_scalar(
+                    out=h_bf[u][:, 0 : 4 * n1].rearrange("p (n t) -> p n t", t=4),
+                    in0=h_rows[u][:, :, 0:n1].rearrange("p t n -> p n t"),
+                    scalar1=1.0,
+                    scalar2=0.0,
+                    op0=ALU.mult,
+                    op1=ALU.add,
+                )
+                return
             nc.vector.tensor_copy(
                 out=h_bf[u][:, 4 * n0 : 4 * n1].rearrange("p (c i t) -> p c t i", i=4, t=4),
                 in_=h_rows[u][:, :, n0:n1].rearrange("p t (c i) -> p c t i", i=4),
@@ -261,7 +271,10 @@ def tile_list_barcode_programme_scores_kernel(
 
         def quantise_h(u, n0, n1):
             if u not in h_codes:
-                h_codes[u] = keep.tile([P, W], U32, name="h_codes%d" % u, align_bytes=64)
+                if u < 2:
+                    h_codes[u] = placed([P, W], U32, "h_codes%d" % u, logs_at[(2, 4)[u]])
+                else:
+                    h_codes[u] = keep.tile([P, W], U32, name="h_codes%d" % u, align_bytes=64)
                 h_scales[u] = keep.tile([P, W], U8, name="h_scales%d" % u, align_bytes=64)
             nc.vector.quantize_mx(
                 out=h_codes[u][:, n0:n1].bitcast(FP8X4),
@@ -289,7 +302,7 @@ def tile_list_barcode_programme_scores_kernel(
             3: [lambda: interleave_h(0, 0, W)],
             6: [lambda: quantise_h(0, 0, W)],
             7: [lambda: interleave_h(1, 0, W)],
-            10: [lambda: quantise_h(1, 0, W)],
+            9: [lambda: quantise_h(1, 0, W)],
         }
 
         for g in range(2):
@@ -300,9 +313,9 @@ def tile_list_barcode_programme_scores_kernel(
                 e_pass(step, 0)
             e_pass(step, 1)
             magnitude(step)
-            if step >= 5:
-                b_pass(step - 1, 0)
-                b_pass(step - 1, 1)
+            if step >= 6:
+                b_pass(step - 2, 0)
+                b_pass(step - 2, 1)
 
         round_we("vector", 1, 0, 0, 0, 128)
         e_pass(0, 0)
@@ -310,34 +323,34 @@ def tile_list_barcode_programme_scores_kernel(
         products(0)
         products(1)
         for pair in range(6):
-            if pair < 5:
+            if pair not in (3, 5):
                 products(2 * pair + 2)
                 logarithm(pair, 0, W)
             else:
                 logarithm(pair, 0, W, 0, 1)
                 logarithm(pair, 0, W, 1, 2)
                 products(2 * pair + 2)
+            products(2 * pair + 3)
             for step in (2 * pair, 2 * pair + 1):
                 correct(step, 0, W)
                 for job in later.get(step, []):
                     job()
-            products(2 * pair + 3)
         products(14)
-        logarithm(6, 0, W)
-        correct(12, 0, W)
-        correct(13, 0, W)
+        logarithm(6, 0, HALF)
         products(15)
-        b_pass(15, 0)
-        b_pass(15, 1)
+        for step in (14, 15):
+            b_pass(step, 0)
+            b_pass(step, 1)
+        logarithm(6, HALF, W)
         logarithm(7, 0, HALF)
         logarithm(7, HALF, W)
-        correct(14, 0, HALF)
-        correct(15, 0, HALF)
+        for step in range(12, 16):
+            correct(step, 0, HALF)
         interleave_h(3, 0, HALF)
-        correct(14, HALF, W)
-        correct(15, HALF, W)
-        quantise_h(3, 0, HALF)
+        for step in range(12, 16):
+            correct(step, HALF, W)
         interleave_h(3, HALF, W)
+        quantise_h(3, 0, HALF)
         quantise_h(3, HALF, W)
 
         out_v = out.rearrange("(n p) j -> p n j", p=P)

@@ -98,13 +98,13 @@ def tile_list_barcode_programme_scores_kernel(
         nc.vector.tensor_copy(out=planes[0][:, 0 : S // 4], in_=picked_scales[:].bitcast(I32))
         for g in range(2):
             for q in range(4):
-                if (g, q) == (1, 3):
+                if (g, q) == (1, 2):
                     load_we(0, 1, 0, HALF, 0)
+                    load_we(0, 1, HALF, HALF, 4 * KB)
                 if (g, q) != (0, 0):
                     nc.sync.dma_start(
                         out=planes[g][32 * q : 32 * q + 4, :], in_=planes[0][16 * g + 4 * q : 16 * g + 4 * q + 4, :]
                     )
-        load_we(0, 1, HALF, HALF, 4 * KB)
         plane_bytes = [pl[:].bitcast(U8) for pl in planes]
 
         wb_codes = {}
@@ -117,22 +117,23 @@ def tile_list_barcode_programme_scores_kernel(
             )
 
         permute_wb(0, 36 * KB)
-        load_wb(1, 17 * KB)
         load_we(1, 0, 0, W, 9 * KB)
         load_we(1, 1, 0, W, 19 * KB)
+        load_wb(1, 17 * KB)
 
         LOGS_AT = 48 * KB
         we_bf, we_codes, we_scales = {}, {}, {}
-        bf_at = {(0, 0): 93 * KB, (0, 1): 88 * KB, (1, 0): 93 * KB, (1, 1): LOGS_AT + 36 * KB}
+        bf_at = {(0, 0): 93 * KB, (0, 1): 88 * KB, (1, 0): 93 * KB, (1, 1): 96 * KB + KB // 2}
         logs_at = [LOGS_AT + 4 * KB * s for s in range(8)]
-        logs_at[0] = bf_at[1, 1]
 
         def round_we(engine, a, g, c0, m0, m1):
             if (a, g) not in we_bf:
                 we_bf[a, g] = placed([P, 4 * W], BF16, "we_bf%d%d" % (a, g), bf_at[a, g])
             dst = we_bf[a, g][:].rearrange("p (t m j) -> p m t j", t=4, j=4)[:, c0 // 4 + m0 : c0 // 4 + m1]
             src = we_raw[a, g, c0][:].rearrange("p j (m t) -> p m t j", t=4)[:, m0:m1]
-            if engine == "scalar":
+            if engine == "gpsimd":
+                nc.gpsimd.tensor_scalar(out=dst, in0=src, scalar1=1.0, scalar2=0.0, op0=ALU.mult, op1=ALU.add)
+            elif engine == "scalar":
                 nc.scalar.copy(out=dst, in_=src)
             else:
                 nc.vector.tensor_copy(out=dst, in_=src)
@@ -151,19 +152,20 @@ def tile_list_barcode_programme_scores_kernel(
                 we_scales[a, g, t] = scales[:, P * (t - t0) : P * (t - t0 + 1)]
 
         v_codes = {}
-        for jt in range(2):
-            picked = placed([P, W], U32, "picked_words%d" % jt, (92 - jt) * KB)
+
+        def pick_cells(jt, at):
+            picked = placed([P, W], U32, "picked_words%d" % jt, at)
             nc.vector.tensor_copy(
                 picked[:], word_win[:].bitcast(U32).indirect(offsets[:, 32 * jt : 32 * (jt + 1)])
             )
-            codes = keep.tile([P, 2, 2 * W], U8, name="v_codes%d" % jt, align_bytes=64)
+            v_codes[jt] = keep.tile([P, 2, 2 * W], U8, name="v_codes%d" % jt, align_bytes=64)
             nc.vector.tensor_copy(
-                out=codes[:].bitcast(U16), in_=picked[:].bitcast(U16).rearrange("p (n g) -> p g n", g=2)
+                out=v_codes[jt][:].bitcast(U16), in_=picked[:].bitcast(U16).rearrange("p (n g) -> p g n", g=2)
             )
-            v_codes[jt] = codes
 
-        round_we("scalar", 0, 0, 0, 0, 96)
-        round_we("vector", 0, 0, 0, 96, 128)
+        pick_cells(0, 91 * KB + KB // 2)
+        round_we("scalar", 0, 0, 0, 0, 72)
+        round_we("vector", 0, 0, 0, 72, 128)
         quantise_we(0, 0, 0, 2)
         round_we("scalar", 0, 1, 0, 0, 64)
         round_we("vector", 0, 1, HALF, 0, 64)
@@ -171,18 +173,20 @@ def tile_list_barcode_programme_scores_kernel(
         quantise_we(0, 1, 1, 2)
         quantise_we(0, 1, 2, 4)
         quantise_we(0, 0, 2, 4, 90 * KB)
-        permute_wb(1, 88 * KB)
+        pick_cells(1, 92 * KB)
 
         w2_codes = placed([P, 2, N], I32, "w2_codes", 0)
         nc.sync.dma_start(out=w2_codes[:], in_=w2_words.rearrange("a p c i -> p a (c i)").bitcast(I32))
-        w2_planes = placed([P, 2, N // 4], I32, "w2_planes", 4 * KB)
-        nc.vector.memset(w2_planes[:], 0)
-        for q in range(4):
-            nc.sync.dma_start(
-                out=w2_planes[32 * q : 32 * q + 4, :, :],
-                in_=w2_scales[:, 4 * q : 4 * q + 4, :].rearrange("a r c -> r a c").bitcast(I32),
-            )
+        w2_planes = placed([P, 2, N // 4], I32, "w2_planes", 100 * KB)
         w2_plane_bytes = w2_planes[:].bitcast(U8)
+
+        def load_w2_scales():
+            nc.vector.memset(w2_planes[:], 0)
+            for q in range(4):
+                nc.sync.dma_start(
+                    out=w2_planes[32 * q : 32 * q + 4, :, :],
+                    in_=w2_scales[:, 4 * q : 4 * q + 4, :].rearrange("a r c -> r a c").bitcast(I32),
+                )
 
         units = [(0, 0), (0, 1), (1, 0), (1, 1)]
         h_rows, h_bf, h_codes, h_scales = {}, {}, {}, {}
@@ -242,7 +246,7 @@ def tile_list_barcode_programme_scores_kernel(
 
         def interleave_h(u, n0, n1):
             if u < 2:
-                h_bf[u] = placed([P, 4 * W], BF16, "h_bf%d" % u, bf_at[1, 1])
+                h_bf[u] = placed([P, 4 * W], BF16, "h_bf%d" % u, 16 * KB)
                 nc.gpsimd.tensor_scalar(
                     out=h_bf[u][:].rearrange("p (n t) -> p n t", t=4),
                     in0=h_rows[u][:].rearrange("p t n -> p n t"),
@@ -272,7 +276,7 @@ def tile_list_barcode_programme_scores_kernel(
         def quantise_h(u, n0, n1):
             if u not in h_codes:
                 if u < 2:
-                    h_codes[u] = placed([P, W], U32, "h_codes%d" % u, logs_at[(2, 4)[u]])
+                    h_codes[u] = placed([P, W], U32, "h_codes%d" % u, logs_at[(2, 5)[u]])
                 else:
                     h_codes[u] = keep.tile([P, W], U32, name="h_codes%d" % u, align_bytes=64)
                 h_scales[u] = keep.tile([P, W], U8, name="h_scales%d" % u, align_bytes=64)
@@ -295,19 +299,19 @@ def tile_list_barcode_programme_scores_kernel(
             )
 
         later = {
-            0: [lambda: quantise_we(1, 0, 0, 4)],
-            1: [lambda: round_we("vector", 1, 1, 0, 0, 128)],
-            2: [lambda: quantise_we(1, 1, 0, 4)],
-            11: [lambda: interleave_h(2, 0, W), lambda: quantise_h(2, 0, W)],
-            3: [lambda: interleave_h(0, 0, W)],
+            11: [lambda: interleave_h(2, 0, W), lambda: quantise_h(1, 0, W), lambda: quantise_h(2, 0, W)],
+            3: [
+                lambda: quantise_we(1, 1, 0, 4, logs_at[1] + 2 * KB),
+                load_w2_scales,
+                lambda: permute_wb(1, logs_at[1]),
+                lambda: interleave_h(0, 0, W),
+            ],
             6: [lambda: quantise_h(0, 0, W)],
             7: [lambda: interleave_h(1, 0, W)],
-            9: [lambda: quantise_h(1, 0, W)],
         }
 
-        for g in range(2):
-            for t in range(4):
-                b_pass(t, g)
+        for t in range(4):
+            b_pass(t, 0)
         def products(step):
             if step >= 2:
                 e_pass(step, 0)
@@ -315,9 +319,12 @@ def tile_list_barcode_programme_scores_kernel(
             magnitude(step)
             if step >= 6:
                 b_pass(step - 2, 0)
+            if step >= 2:
                 b_pass(step - 2, 1)
 
         round_we("vector", 1, 0, 0, 0, 128)
+        quantise_we(1, 0, 0, 4)
+        round_we("gpsimd", 1, 1, 0, 0, 128)
         e_pass(0, 0)
         e_pass(1, 0)
         products(0)

@@ -117,26 +117,27 @@ def tile_list_barcode_programme_scores_kernel(
             )
 
         permute_wb(0, 36 * KB)
+        load_wb(1, 17 * KB)
         load_we(1, 0, 0, W, 9 * KB)
         load_we(1, 1, 0, W, 19 * KB)
-        load_wb(1, 17 * KB)
 
         LOGS_AT = 48 * KB
         we_bf, we_codes, we_scales = {}, {}, {}
         bf_at = {(0, 0): 93 * KB, (0, 1): 88 * KB, (1, 0): 93 * KB, (1, 1): 96 * KB + KB // 2}
         logs_at = [LOGS_AT + 4 * KB * s for s in range(8)]
+        logs_at[0] = bf_at[1, 1] + KB
 
         def round_we(engine, a, g, c0, m0, m1):
             if (a, g) not in we_bf:
                 we_bf[a, g] = placed([P, 4 * W], BF16, "we_bf%d%d" % (a, g), bf_at[a, g])
             dst = we_bf[a, g][:].rearrange("p (t m j) -> p m t j", t=4, j=4)[:, c0 // 4 + m0 : c0 // 4 + m1]
             src = we_raw[a, g, c0][:].rearrange("p j (m t) -> p m t j", t=4)[:, m0:m1]
-            if engine == "gpsimd":
-                nc.gpsimd.tensor_scalar(out=dst, in0=src, scalar1=1.0, scalar2=0.0, op0=ALU.mult, op1=ALU.add)
-            elif engine == "scalar":
+            if engine == "scalar":
                 nc.scalar.copy(out=dst, in_=src)
             else:
                 nc.vector.tensor_copy(out=dst, in_=src)
+
+        we_planes = [keep.tile([P, 2, W], U8, name="we_planes%d" % a, align_bytes=64) for a in range(2)]
 
         def quantise_we(a, g, t0, t1, at=None):
             name = "%d%d%d" % (a, g, t0)
@@ -145,8 +146,8 @@ def tile_list_barcode_programme_scores_kernel(
                 codes = keep.tile([P, width], U32, name="we_codes" + name, align_bytes=64)
             else:
                 codes = placed([P, width], U32, "we_codes" + name, at)
-            scales = keep.tile([P, width], U8, name="we_scales" + name, align_bytes=64)
-            nc.vector.quantize_mx(out=codes[:].bitcast(FP8X4), scales=scales[:], in_=we_bf[a, g][:, W * t0 : W * t1])
+            scales = we_planes[a][:, g, P * t0 : P * t1]
+            nc.vector.quantize_mx(out=codes[:].bitcast(FP8X4), scales=scales, in_=we_bf[a, g][:, W * t0 : W * t1])
             for t in range(t0, t1):
                 we_codes[a, g, t] = codes[:, P * (t - t0) : P * (t - t0 + 1)]
                 we_scales[a, g, t] = scales[:, P * (t - t0) : P * (t - t0 + 1)]
@@ -177,11 +178,10 @@ def tile_list_barcode_programme_scores_kernel(
 
         w2_codes = placed([P, 2, N], I32, "w2_codes", 0)
         nc.sync.dma_start(out=w2_codes[:], in_=w2_words.rearrange("a p c i -> p a (c i)").bitcast(I32))
-        w2_planes = placed([P, 2, N // 4], I32, "w2_planes", 100 * KB)
-        w2_plane_bytes = w2_planes[:].bitcast(U8)
+        w2_planes = we_planes[0][:].bitcast(I32)
+        w2_plane_bytes = we_planes[0][:]
 
         def load_w2_scales():
-            nc.vector.memset(w2_planes[:], 0)
             for q in range(4):
                 nc.sync.dma_start(
                     out=w2_planes[32 * q : 32 * q + 4, :, :],
@@ -246,7 +246,7 @@ def tile_list_barcode_programme_scores_kernel(
 
         def interleave_h(u, n0, n1):
             if u < 2:
-                h_bf[u] = placed([P, 4 * W], BF16, "h_bf%d" % u, 16 * KB)
+                h_bf[u] = placed([P, 4 * W], BF16, "h_bf%d" % u, bf_at[1, 1])
                 nc.gpsimd.tensor_scalar(
                     out=h_bf[u][:].rearrange("p (n t) -> p n t", t=4),
                     in0=h_rows[u][:].rearrange("p t n -> p n t"),
@@ -300,12 +300,10 @@ def tile_list_barcode_programme_scores_kernel(
 
         later = {
             11: [lambda: interleave_h(2, 0, W), lambda: quantise_h(1, 0, W), lambda: quantise_h(2, 0, W)],
-            3: [
-                lambda: quantise_we(1, 1, 0, 4, logs_at[1] + 2 * KB),
-                load_w2_scales,
-                lambda: permute_wb(1, logs_at[1]),
-                lambda: interleave_h(0, 0, W),
-            ],
+            1: [lambda: round_we("vector", 1, 1, 0, 0, 128)],
+            2: [lambda: quantise_we(1, 1, 0, 4)],
+            3: [lambda: interleave_h(0, 0, W)],
+            5: [load_w2_scales],
             6: [lambda: quantise_h(0, 0, W)],
             7: [lambda: interleave_h(1, 0, W)],
         }
@@ -323,8 +321,8 @@ def tile_list_barcode_programme_scores_kernel(
                 b_pass(step - 2, 1)
 
         round_we("vector", 1, 0, 0, 0, 128)
+        permute_wb(1, 91 * KB)
         quantise_we(1, 0, 0, 4)
-        round_we("gpsimd", 1, 1, 0, 0, 128)
         e_pass(0, 0)
         e_pass(1, 0)
         products(0)

@@ -98,13 +98,13 @@ def tile_list_barcode_programme_scores_kernel(
         nc.vector.tensor_copy(out=planes[0][:, 0 : S // 4], in_=picked_scales[:].bitcast(I32))
         for g in range(2):
             for q in range(4):
-                if (g, q) == (1, 2):
+                if (g, q) == (1, 3):
                     load_we(0, 1, 0, HALF, 0)
-                    load_we(0, 1, HALF, HALF, 4 * KB)
                 if (g, q) != (0, 0):
                     nc.sync.dma_start(
                         out=planes[g][32 * q : 32 * q + 4, :], in_=planes[0][16 * g + 4 * q : 16 * g + 4 * q + 4, :]
                     )
+        load_we(0, 1, HALF, HALF, 4 * KB)
         plane_bytes = [pl[:].bitcast(U8) for pl in planes]
 
         wb_codes = {}
@@ -123,7 +123,7 @@ def tile_list_barcode_programme_scores_kernel(
 
         LOGS_AT = 48 * KB
         we_bf, we_codes, we_scales = {}, {}, {}
-        bf_at = {(0, 0): 93 * KB, (0, 1): 88 * KB, (1, 0): 93 * KB, (1, 1): 96 * KB + KB // 2}
+        bf_at = {(0, 0): 93 * KB, (0, 1): 88 * KB, (1, 0): 94 * KB, (1, 1): 97 * KB + KB // 2}
         logs_at = [LOGS_AT + 4 * KB * s for s in range(8)]
         logs_at[0] = bf_at[1, 1] + KB
 
@@ -159,14 +159,19 @@ def tile_list_barcode_programme_scores_kernel(
             nc.vector.tensor_copy(
                 picked[:], word_win[:].bitcast(U32).indirect(offsets[:, 32 * jt : 32 * (jt + 1)])
             )
+            return picked
+
+        def part_cells(jt, picked):
             v_codes[jt] = keep.tile([P, 2, 2 * W], U8, name="v_codes%d" % jt, align_bytes=64)
             nc.vector.tensor_copy(
                 out=v_codes[jt][:].bitcast(U16), in_=picked[:].bitcast(U16).rearrange("p (n g) -> p g n", g=2)
             )
 
-        pick_cells(0, 91 * KB + KB // 2)
-        round_we("scalar", 0, 0, 0, 0, 72)
-        round_we("vector", 0, 0, 0, 72, 128)
+        part_cells(0, pick_cells(0, 92 * KB))
+        picked = pick_cells(1, 91 * KB)
+        round_we("scalar", 0, 0, 0, 0, 96)
+        round_we("vector", 0, 0, 0, 96, 128)
+        part_cells(1, picked)
         quantise_we(0, 0, 0, 2)
         round_we("scalar", 0, 1, 0, 0, 64)
         round_we("vector", 0, 1, HALF, 0, 64)
@@ -174,7 +179,6 @@ def tile_list_barcode_programme_scores_kernel(
         quantise_we(0, 1, 1, 2)
         quantise_we(0, 1, 2, 4)
         quantise_we(0, 0, 2, 4, 90 * KB)
-        pick_cells(1, 92 * KB)
 
         w2_codes = placed([P, 2, N], I32, "w2_codes", 0)
         nc.sync.dma_start(out=w2_codes[:], in_=w2_words.rearrange("a p c i -> p a (c i)").bitcast(I32))
@@ -308,8 +312,10 @@ def tile_list_barcode_programme_scores_kernel(
             7: [lambda: interleave_h(1, 0, W)],
         }
 
-        for t in range(4):
-            b_pass(t, 0)
+        for g in range(2):
+            for t in range(4):
+                b_pass(t, g)
+
         def products(step):
             if step >= 2:
                 e_pass(step, 0)
@@ -317,11 +323,10 @@ def tile_list_barcode_programme_scores_kernel(
             magnitude(step)
             if step >= 6:
                 b_pass(step - 2, 0)
-            if step >= 2:
                 b_pass(step - 2, 1)
 
         round_we("vector", 1, 0, 0, 0, 128)
-        permute_wb(1, 91 * KB)
+        permute_wb(1, 91 * KB + KB // 2)
         quantise_we(1, 0, 0, 4)
         e_pass(0, 0)
         e_pass(1, 0)

@@ -130,8 +130,8 @@ def tile_list_barcode_programme_scores_kernel(
         def round_we(engine, a, g, c0, m0, m1):
             if (a, g) not in we_bf:
                 we_bf[a, g] = placed([P, 4 * W], BF16, "we_bf%d%d" % (a, g), bf_at[a, g])
-            dst = we_bf[a, g][:].rearrange("p (t m j) -> p m t j", t=4, j=4)[:, c0 // 4 + m0 : c0 // 4 + m1]
-            src = we_raw[a, g, c0][:].rearrange("p j (m t) -> p m t j", t=4)[:, m0:m1]
+            dst = we_bf[a, g][:].rearrange("p (t m j) -> p m j t", t=4, j=4)[:, c0 // 4 + m0 : c0 // 4 + m1]
+            src = we_raw[a, g, c0][:].rearrange("p j (m t) -> p m j t", t=4)[:, m0:m1]
             if engine == "scalar":
                 nc.scalar.copy(out=dst, in_=src)
             else:

@@ -45,11 +45,9 @@ def tile_list_barcode_programme_scores_kernel(
         word_win = keep.tile([P, T], I32, name="word_win", align_bytes=64)
         planes = [keep.tile([P, PLANE // 4], I32, name="plane%d" % g, align_bytes=64) for g in range(2)]
         wb_rows = keep.tile([P, H // 4], I32, name="wb_rows", align_bytes=64)
-        gain_sb = keep.tile([P, 2, 4], F32, name="gain_sb")
         one = keep.tile([P, 1], F32, name="one")
         zero = keep.tile([P, 1], F32, name="zero")
 
-        nc.scalar.dma_start(out=gain_sb[:], in_=gain.rearrange("(a p t) -> p a t", a=2, t=4))
         nc.vector.memset(one[:], 1.0)
         nc.scalar.activation(out=zero[:], in_=one[:], func=ACT.Ln)
         nc.vector.memset(scale_win[32:64, :], 0)
@@ -68,7 +66,7 @@ def tile_list_barcode_programme_scores_kernel(
         wb_raw, we_raw = {}, {}
 
         def load_wb(a, at):
-            held = placed([P, W + (32 if a == 0 else 0)], I32, "wb_raw%d" % a, at)
+            held = placed([P, W], I32, "wb_raw%d" % a, at)
             wb_raw[a] = held[:, 0:W].rearrange("p (g b) -> p g b", g=2)
             nc.sync.dma_start(
                 out=wb_raw[a],
@@ -83,13 +81,15 @@ def tile_list_barcode_programme_scores_kernel(
             )
             we_raw[a, g, c0] = raw
 
-        load_wb(0, 17 * KB - 64)
+        load_wb(0, 17 * KB)
         nc.sync.dma_start(
             out=word_win[:], in_=tab[0, 0 : 512 * T].rearrange("(p b) -> p b", p=P).bitcast(I32)
         )
         load_we(0, 0, 0, W, 28 * KB)
+        load_we(0, 1, 0, HALF, 0)
+        load_we(0, 1, HALF, HALF, 4 * KB)
 
-        picked_scales = placed([P, S], U8, "picked_scales", 4 * KB - KB // 2)
+        picked_scales = keep.tile([P, S], U8, name="picked_scales", align_bytes=64)
         nc.vector.tensor_copy(picked_scales[:], scale_win[:].bitcast(U8).indirect(offsets[:]))
         nc.vector.tensor_copy(
             out=planes[0][:].bitcast(U8)[:, WB_AT:PLANE].rearrange("p (a t m) -> p a t m", a=2, t=4),
@@ -98,13 +98,11 @@ def tile_list_barcode_programme_scores_kernel(
         nc.vector.tensor_copy(out=planes[0][:, 0 : S // 4], in_=picked_scales[:].bitcast(I32))
         for g in range(2):
             for q in range(4):
-                if (g, q) == (1, 3):
-                    load_we(0, 1, 0, HALF, 0)
                 if (g, q) != (0, 0):
-                    nc.sync.dma_start(
+                    queue = nc.gpsimd if (g, q) >= (1, 2) else nc.scalar
+                    queue.dma_start(
                         out=planes[g][32 * q : 32 * q + 4, :], in_=planes[0][16 * g + 4 * q : 16 * g + 4 * q + 4, :]
                     )
-        load_we(0, 1, HALF, HALF, 4 * KB)
         plane_bytes = [pl[:].bitcast(U8) for pl in planes]
 
         wb_codes = {}
@@ -117,9 +115,6 @@ def tile_list_barcode_programme_scores_kernel(
             )
 
         permute_wb(0, 36 * KB)
-        load_wb(1, 17 * KB)
-        load_we(1, 0, 0, W, 9 * KB)
-        load_we(1, 1, 0, W, 19 * KB)
 
         LOGS_AT = 48 * KB
         we_bf, we_codes, we_scales = {}, {}, {}
@@ -154,29 +149,34 @@ def tile_list_barcode_programme_scores_kernel(
 
         v_codes = {}
 
-        def pick_cells(jt, at):
-            picked = placed([P, W], U32, "picked_words%d" % jt, at)
+        def pick_cells(jt, at, span, skip):
+            held = placed([P, span // 4], U32, "picked_words%d" % jt, at)
+            picked = held[:, skip // 4 : skip // 4 + W]
             nc.vector.tensor_copy(
-                picked[:], word_win[:].bitcast(U32).indirect(offsets[:, 32 * jt : 32 * (jt + 1)])
+                picked, word_win[:].bitcast(U32).indirect(offsets[:, 32 * jt : 32 * (jt + 1)])
             )
             return picked
 
         def part_cells(jt, picked):
             v_codes[jt] = keep.tile([P, 2, 2 * W], U8, name="v_codes%d" % jt, align_bytes=64)
             nc.vector.tensor_copy(
-                out=v_codes[jt][:].bitcast(U16), in_=picked[:].bitcast(U16).rearrange("p (n g) -> p g n", g=2)
+                out=v_codes[jt][:].bitcast(U16), in_=picked.bitcast(U16).rearrange("p (n g) -> p g n", g=2)
             )
 
-        part_cells(0, pick_cells(0, 92 * KB))
-        picked = pick_cells(1, 91 * KB)
-        round_we("scalar", 0, 0, 0, 0, 96)
-        round_we("vector", 0, 0, 0, 96, 128)
+        part_cells(0, pick_cells(0, 92 * KB, 12 * KB, 0))
+        load_we(1, 0, 0, W, 103 * KB + KB // 2)
+        gain_sb = placed([P, 2, 4], F32, "gain_sb", 103 * KB)
+        nc.sync.dma_start(out=gain_sb[:], in_=gain.rearrange("(a p t) -> p a t", a=2, t=4))
+        picked = pick_cells(1, 78 * KB, 15 * KB, 13 * KB)
+        round_we("scalar", 0, 0, 0, 0, 112)
         part_cells(1, picked)
-        quantise_we(0, 0, 0, 2)
-        round_we("scalar", 0, 1, 0, 0, 64)
+        load_wb(1, 78 * KB)
+        load_we(1, 1, 0, W, 80 * KB)
+        round_we("vector", 0, 0, 0, 112, 128)
+        round_we("vector", 0, 1, 0, 0, 64)
         round_we("vector", 0, 1, HALF, 0, 64)
-        quantise_we(0, 1, 0, 1)
-        quantise_we(0, 1, 1, 2)
+        quantise_we(0, 0, 0, 2)
+        quantise_we(0, 1, 0, 2)
         quantise_we(0, 1, 2, 4)
         quantise_we(0, 0, 2, 4, 90 * KB)
 

@@ -19,9 +19,36 @@ ALU = mybir.AluOpType
 P = 128
 W = 512
 HALF = W // 2
+QUARTER = W // 4
 ROWS = 32
 V_AT, WB_AT, PLANE = 0, S, S + H
 KB = 1024
+
+SCALAR_GROUPS = 112
+FIRST_GPSIMD_MOVE = (1, 2)
+
+WE_RAW_AT = {
+    (0, 1, 0): 0,
+    (0, 1, HALF): 4 * KB,
+    (0, 0, 0): 28 * KB,
+    (1, 1, 0): 80 * KB,
+    (1, 0, 0): 103 * KB + KB // 2,
+}
+W2_CODES_AT = 0
+WB_RAW_AT = (17 * KB, 78 * KB)
+WB_CODES_AT = (36 * KB, 91 * KB + KB // 2)
+GAIN_AT = 103 * KB
+PICKED_AT = ((92 * KB, 12 * KB, 0), (78 * KB, 15 * KB, 13 * KB))
+WE_BF_AT = {
+    (0, 0): 93 * KB,
+    (0, 1): 88 * KB,
+    (1, 0): 94 * KB,
+    (1, 1): 97 * KB + KB // 2,
+}
+LATE_CODES_AT = 90 * KB
+LOGS_AT = [WE_BF_AT[1, 1] + KB] + [48 * KB + 4 * KB * pair for pair in range(1, 8)]
+EARLY_H_BF_AT = WE_BF_AT[1, 1]
+EARLY_H_CODES_AT = (LOGS_AT[2], LOGS_AT[5])
 
 
 def tile_list_barcode_programme_scores_kernel(
@@ -65,29 +92,29 @@ def tile_list_barcode_programme_scores_kernel(
 
         wb_raw, we_raw = {}, {}
 
-        def load_wb(a, at):
-            held = placed([P, W], I32, "wb_raw%d" % a, at)
-            wb_raw[a] = held[:, 0:W].rearrange("p (g b) -> p g b", g=2)
+        def load_wb(a):
+            raw = placed([P, W], I32, "wb_raw%d" % a, WB_RAW_AT[a])
+            wb_raw[a] = raw[:].rearrange("p (g b) -> p g b", g=2)
             nc.sync.dma_start(
                 out=wb_raw[a],
                 in_=wb_words[:, :, 2 * W * a : 2 * W * (a + 1)].rearrange("g p b -> p g b").bitcast(I32),
             )
 
-        def load_we(a, g, c0, cw, at):
-            raw = placed([P, 4, cw], F32, "we_raw%d%d_%d" % (a, g, c0), at)
+        def load_we(a, g, c0, cw):
+            raw = placed([P, 4, cw], F32, "we_raw%d%d_%d" % (a, g, c0), WE_RAW_AT[a, g, c0])
             nc.sync.dma_start(
                 out=raw[:],
                 in_=we[W * g : W * (g + 1), W * a + c0 : W * a + c0 + cw].rearrange("(p j) c -> p j c", j=4),
             )
             we_raw[a, g, c0] = raw
 
-        load_wb(0, 17 * KB)
+        load_wb(0)
         nc.sync.dma_start(
             out=word_win[:], in_=tab[0, 0 : 512 * T].rearrange("(p b) -> p b", p=P).bitcast(I32)
         )
-        load_we(0, 0, 0, W, 28 * KB)
-        load_we(0, 1, 0, HALF, 0)
-        load_we(0, 1, HALF, HALF, 4 * KB)
+        load_we(0, 0, 0, W)
+        load_we(0, 1, 0, HALF)
+        load_we(0, 1, HALF, HALF)
 
         picked_scales = keep.tile([P, S], U8, name="picked_scales", align_bytes=64)
         nc.vector.tensor_copy(picked_scales[:], scale_win[:].bitcast(U8).indirect(offsets[:]))
@@ -99,7 +126,7 @@ def tile_list_barcode_programme_scores_kernel(
         for g in range(2):
             for q in range(4):
                 if (g, q) != (0, 0):
-                    queue = nc.gpsimd if (g, q) >= (1, 2) else nc.scalar
+                    queue = nc.gpsimd if (g, q) >= FIRST_GPSIMD_MOVE else nc.scalar
                     queue.dma_start(
                         out=planes[g][32 * q : 32 * q + 4, :], in_=planes[0][16 * g + 4 * q : 16 * g + 4 * q + 4, :]
                     )
@@ -107,24 +134,20 @@ def tile_list_barcode_programme_scores_kernel(
 
         wb_codes = {}
 
-        def permute_wb(a, at):
-            wb_codes[a] = placed([P, 2, 2 * W], U8, "wb_codes%d" % a, at)
+        def permute_wb(a):
+            wb_codes[a] = placed([P, 2, 2 * W], U8, "wb_codes%d" % a, WB_CODES_AT[a])
             nc.vector.tensor_copy(
                 out=wb_codes[a][:].bitcast(U16).rearrange("p g (t m) -> p g t m", t=4),
                 in_=wb_raw[a].bitcast(U16).rearrange("p g (m t) -> p g t m", t=4),
             )
 
-        permute_wb(0, 36 * KB)
+        permute_wb(0)
 
-        LOGS_AT = 48 * KB
         we_bf, we_codes, we_scales = {}, {}, {}
-        bf_at = {(0, 0): 93 * KB, (0, 1): 88 * KB, (1, 0): 94 * KB, (1, 1): 97 * KB + KB // 2}
-        logs_at = [LOGS_AT + 4 * KB * s for s in range(8)]
-        logs_at[0] = bf_at[1, 1] + KB
 
         def round_we(engine, a, g, c0, m0, m1):
             if (a, g) not in we_bf:
-                we_bf[a, g] = placed([P, 4 * W], BF16, "we_bf%d%d" % (a, g), bf_at[a, g])
+                we_bf[a, g] = placed([P, 4 * W], BF16, "we_bf%d%d" % (a, g), WE_BF_AT[a, g])
             dst = we_bf[a, g][:].rearrange("p (t m j) -> p m j t", t=4, j=4)[:, c0 // 4 + m0 : c0 // 4 + m1]
             src = we_raw[a, g, c0][:].rearrange("p j (m t) -> p m j t", t=4)[:, m0:m1]
             if engine == "scalar":
@@ -149,11 +172,12 @@ def tile_list_barcode_programme_scores_kernel(
 
         v_codes = {}
 
-        def pick_cells(jt, at, span, skip):
+        def pick_cells(jt):
+            at, span, skip = PICKED_AT[jt]
             held = placed([P, span // 4], U32, "picked_words%d" % jt, at)
             picked = held[:, skip // 4 : skip // 4 + W]
             nc.vector.tensor_copy(
-                picked, word_win[:].bitcast(U32).indirect(offsets[:, 32 * jt : 32 * (jt + 1)])
+                picked, word_win[:].bitcast(U32).indirect(offsets[:, W // 16 * jt : W // 16 * (jt + 1)])
             )
             return picked
 
@@ -163,24 +187,24 @@ def tile_list_barcode_programme_scores_kernel(
                 out=v_codes[jt][:].bitcast(U16), in_=picked.bitcast(U16).rearrange("p (n g) -> p g n", g=2)
             )
 
-        part_cells(0, pick_cells(0, 92 * KB, 12 * KB, 0))
-        load_we(1, 0, 0, W, 103 * KB + KB // 2)
-        gain_sb = placed([P, 2, 4], F32, "gain_sb", 103 * KB)
+        part_cells(0, pick_cells(0))
+        load_we(1, 0, 0, W)
+        gain_sb = placed([P, 2, 4], F32, "gain_sb", GAIN_AT)
         nc.sync.dma_start(out=gain_sb[:], in_=gain.rearrange("(a p t) -> p a t", a=2, t=4))
-        picked = pick_cells(1, 78 * KB, 15 * KB, 13 * KB)
-        round_we("scalar", 0, 0, 0, 0, 112)
+        picked = pick_cells(1)
+        round_we("scalar", 0, 0, 0, 0, SCALAR_GROUPS)
         part_cells(1, picked)
-        load_wb(1, 78 * KB)
-        load_we(1, 1, 0, W, 80 * KB)
-        round_we("vector", 0, 0, 0, 112, 128)
-        round_we("vector", 0, 1, 0, 0, 64)
-        round_we("vector", 0, 1, HALF, 0, 64)
+        load_wb(1)
+        load_we(1, 1, 0, W)
+        round_we("vector", 0, 0, 0, SCALAR_GROUPS, W // 4)
+        round_we("vector", 0, 1, 0, 0, HALF // 4)
+        round_we("vector", 0, 1, HALF, 0, HALF // 4)
         quantise_we(0, 0, 0, 2)
         quantise_we(0, 1, 0, 2)
         quantise_we(0, 1, 2, 4)
-        quantise_we(0, 0, 2, 4, 90 * KB)
+        quantise_we(0, 0, 2, 4, LATE_CODES_AT)
 
-        w2_codes = placed([P, 2, N], I32, "w2_codes", 0)
+        w2_codes = placed([P, 2, N], I32, "w2_codes", W2_CODES_AT)
         nc.sync.dma_start(out=w2_codes[:], in_=w2_words.rearrange("a p c i -> p a (c i)").bitcast(I32))
         w2_planes = we_planes[0][:].bitcast(I32)
         w2_plane_bytes = we_planes[0][:]
@@ -228,12 +252,19 @@ def tile_list_barcode_programme_scores_kernel(
         def magnitude(step):
             if step % 2 == 0:
                 mags[step // 2] = ring.tile([P, 2, W], F32, name="mag%d" % step, tag="mag", bufs=3)
-            nc.scalar.activation(out=mags[step // 2][:, step % 2, :], in_=e_ps[step][:], func=ACT.Abs, bias=zero[:])
+            nc.scalar.activation(
+                out=mags[step // 2][:, step % 2, :],
+                in_=e_ps[step][:],
+                func=ACT.Abs,
+                bias=zero[:] if step == 0 else 0.0,
+            )
 
         def logarithm(pair, n0, n1, k0=0, k1=2):
             if pair not in logs:
-                logs[pair] = placed([P, 2, W], F32, "logs%d" % pair, logs_at[pair])
-            nc.scalar.activation(out=logs[pair][:, k0:k1, n0:n1], in_=mags[pair][:, k0:k1, n0:n1], func=ACT.Ln, bias=1.0)
+                logs[pair] = placed([P, 2, W], F32, "logs%d" % pair, LOGS_AT[pair])
+            nc.scalar.activation(
+                out=logs[pair][:, k0:k1, n0:n1], in_=mags[pair][:, k0:k1, n0:n1], func=ACT.Ln, bias=1.0
+            )
 
         def correct(step, n0, n1):
             u, t = divmod(step, 4)
@@ -248,39 +279,32 @@ def tile_list_barcode_programme_scores_kernel(
                 op1=ALU.subtract,
             )
 
-        def interleave_h(u, n0, n1):
-            if u < 2:
-                h_bf[u] = placed([P, 4 * W], BF16, "h_bf%d" % u, bf_at[1, 1])
-                nc.gpsimd.tensor_scalar(
-                    out=h_bf[u][:].rearrange("p (n t) -> p n t", t=4),
-                    in0=h_rows[u][:].rearrange("p t n -> p n t"),
-                    scalar1=1.0,
-                    scalar2=0.0,
-                    op0=ALU.mult,
-                    op1=ALU.add,
-                )
-                return
+        def interleave_h(engine, u, n0, n1):
             if u not in h_bf:
-                h_bf[u] = ring.tile([P, 4 * W], BF16, name="h_bf%d" % u, tag="h_bf", align_bytes=64)
-            if (u, n0) == (3, 0):
+                if u < 2:
+                    h_bf[u] = placed([P, 4 * W], BF16, "h_bf%d" % u, EARLY_H_BF_AT)
+                else:
+                    h_bf[u] = ring.tile([P, 4 * W], BF16, name="h_bf%d" % u, tag="h_bf", align_bytes=64)
+            dst, src = h_bf[u][:, 4 * n0 : 4 * n1], h_rows[u][:, :, n0:n1]
+            if engine == "gpsimd":
                 nc.gpsimd.tensor_scalar(
-                    out=h_bf[u][:, 0 : 4 * n1].rearrange("p (n t) -> p n t", t=4),
-                    in0=h_rows[u][:, :, 0:n1].rearrange("p t n -> p n t"),
+                    out=dst.rearrange("p (n t) -> p n t", t=4),
+                    in0=src.rearrange("p t n -> p n t"),
                     scalar1=1.0,
                     scalar2=0.0,
                     op0=ALU.mult,
                     op1=ALU.add,
                 )
-                return
-            nc.vector.tensor_copy(
-                out=h_bf[u][:, 4 * n0 : 4 * n1].rearrange("p (c i t) -> p c t i", i=4, t=4),
-                in_=h_rows[u][:, :, n0:n1].rearrange("p t (c i) -> p c t i", i=4),
-            )
+            else:
+                nc.vector.tensor_copy(
+                    out=dst.rearrange("p (c i t) -> p c t i", i=4, t=4),
+                    in_=src.rearrange("p t (c i) -> p c t i", i=4),
+                )
 
         def quantise_h(u, n0, n1):
             if u not in h_codes:
                 if u < 2:
-                    h_codes[u] = placed([P, W], U32, "h_codes%d" % u, logs_at[(2, 5)[u]])
+                    h_codes[u] = placed([P, W], U32, "h_codes%d" % u, EARLY_H_CODES_AT[u])
                 else:
                     h_codes[u] = keep.tile([P, W], U32, name="h_codes%d" % u, align_bytes=64)
                 h_scales[u] = keep.tile([P, W], U8, name="h_scales%d" % u, align_bytes=64)
@@ -303,13 +327,13 @@ def tile_list_barcode_programme_scores_kernel(
             )
 
         later = {
-            11: [lambda: interleave_h(2, 0, W), lambda: quantise_h(1, 0, W), lambda: quantise_h(2, 0, W)],
-            1: [lambda: round_we("vector", 1, 1, 0, 0, 128)],
+            1: [lambda: round_we("vector", 1, 1, 0, 0, W // 4)],
             2: [lambda: quantise_we(1, 1, 0, 4)],
-            3: [lambda: interleave_h(0, 0, W)],
+            3: [lambda: interleave_h("gpsimd", 0, 0, W)],
             5: [load_w2_scales],
             6: [lambda: quantise_h(0, 0, W)],
-            7: [lambda: interleave_h(1, 0, W)],
+            7: [lambda: interleave_h("gpsimd", 1, 0, W)],
+            11: [lambda: interleave_h("vector", 2, 0, W), lambda: quantise_h(1, 0, W), lambda: quantise_h(2, 0, W)],
         }
 
         for g in range(2):
@@ -325,8 +349,8 @@ def tile_list_barcode_programme_scores_kernel(
                 b_pass(step - 2, 0)
                 b_pass(step - 2, 1)
 
-        round_we("vector", 1, 0, 0, 0, 128)
-        permute_wb(1, 91 * KB + KB // 2)
+        round_we("vector", 1, 0, 0, 0, W // 4)
+        permute_wb(1)
         quantise_we(1, 0, 0, 4)
         e_pass(0, 0)
         e_pass(1, 0)
@@ -351,17 +375,19 @@ def tile_list_barcode_programme_scores_kernel(
         for step in (14, 15):
             b_pass(step, 0)
             b_pass(step, 1)
-        logarithm(6, HALF, W)
         logarithm(7, 0, HALF)
+        logarithm(6, HALF, W)
         logarithm(7, HALF, W)
         for step in range(12, 16):
             correct(step, 0, HALF)
-        interleave_h(3, 0, HALF)
+        interleave_h("gpsimd", 3, 0, HALF)
         for step in range(12, 16):
             correct(step, HALF, W)
-        interleave_h(3, HALF, W)
         quantise_h(3, 0, HALF)
-        quantise_h(3, HALF, W)
+        interleave_h("vector", 3, HALF, HALF + QUARTER)
+        interleave_h("vector", 3, HALF + QUARTER, W)
+        quantise_h(3, HALF, HALF + QUARTER)
+        quantise_h(3, HALF + QUARTER, W)
 
         out_v = out.rearrange("(n p) j -> p n j", p=P)
         first = [bank(n, "o_ps%d" % n) for n in range(4)]
@@ -372,17 +398,33 @@ def tile_list_barcode_programme_scores_kernel(
             res = keep.tile([P, W], F32, name="res0_%d" % n)
             nc.scalar.copy(out=res[:], in_=first[n][:])
             nc.sync.dma_start(out=out_v[:, n, 0:W], in_=res[:])
-        for half in range(2):
-            pairs = [bank(4 + 2 * half + pair, "o_ps%d%d" % (half, pair)) for pair in range(2)]
-            for a in range(2):
-                for n in range(4):
-                    dst = pairs[n // 2][:, HALF * (n % 2) : HALF * (n % 2 + 1)]
-                    score_pass(dst, n, 1, a, HALF * half, HALF * (half + 1), (a, n % 2) == (0, 0), (a, n % 2) == (1, 1))
-            for pair in range(2):
-                res = keep.tile([P, 2, HALF], F32, name="res1_%d%d" % (half, pair))
-                if pair == 0:
-                    nc.vector.tensor_copy(out=res[:].rearrange("p k j -> p (k j)"), in_=pairs[pair][:])
+        parts = [
+            (0, HALF, (4, 5), ("scalar", "scalar")),
+            (HALF, QUARTER, (6,), ("vector",)),
+            (HALF + QUARTER, QUARTER, (7, 0), ("scalar", "vector")),
+        ]
+        part_ps = [[bank(i, "o_ps%d_%d" % (c0, i)) for i in banks] for c0, cells, banks, engines in parts]
+
+        def part_passes(k, a):
+            c0, cells, banks, engines = parts[k]
+            per_bank = 4 // len(banks)
+            for n in range(4):
+                i, j = divmod(n, per_bank)
+                dst = part_ps[k][i][:, cells * j : cells * (j + 1)]
+                score_pass(dst, n, 1, a, c0, c0 + cells, (a, j) == (0, 0), (a, j) == (1, per_bank - 1))
+
+        for k in range(len(parts)):
+            part_passes(k, 0)
+        for k, (c0, cells, banks, engines) in enumerate(parts):
+            part_passes(k, 1)
+            per_bank = 4 // len(banks)
+            for i, engine in enumerate(engines):
+                res = keep.tile([P, per_bank, cells], F32, name="res1_%d%d" % (k, i))
+                src = part_ps[k][i][:, 0 : per_bank * cells]
+                if engine == "vector":
+                    nc.vector.tensor_copy(out=res[:].rearrange("p k j -> p (k j)"), in_=src)
                 else:
-                    nc.scalar.copy(out=res[:].rearrange("p k j -> p (k j)"), in_=pairs[pair][:])
-                c0 = W + HALF * half
-                nc.sync.dma_start(out=out_v[:, 2 * pair : 2 * pair + 2, c0 : c0 + HALF], in_=res[:])
+                    nc.scalar.copy(out=res[:].rearrange("p k j -> p (k j)"), in_=src)
+                nc.sync.dma_start(
+                    out=out_v[:, per_bank * i : per_bank * (i + 1), W + c0 : W + c0 + cells], in_=res[:]
+                )

@@ -19,36 +19,41 @@ ALU = mybir.AluOpType
 P = 128
 W = 512
 HALF = W // 2
-QUARTER = W // 4
 ROWS = 32
 V_AT, WB_AT, PLANE = 0, S, S + H
 KB = 1024
 
-SCALAR_GROUPS = 112
-FIRST_GPSIMD_MOVE = (1, 2)
+SCALAR_GROUPS_FIRST = 44
+SCALAR_GROUPS_LAST = 20
+GPSIMD_MOVE = (1, 3)
 
 WE_RAW_AT = {
     (0, 1, 0): 0,
-    (0, 1, HALF): 4 * KB,
-    (0, 0, 0): 28 * KB,
-    (1, 1, 0): 80 * KB,
-    (1, 0, 0): 103 * KB + KB // 2,
+    (0, 1, HALF): 10 * KB,
+    (0, 0, 0): 16 * KB,
+    (1, 0, 0): 32 * KB + KB // 2,
+    (1, 1, 0): 45 * KB,
 }
 W2_CODES_AT = 0
-WB_RAW_AT = (17 * KB, 78 * KB)
-WB_CODES_AT = (36 * KB, 91 * KB + KB // 2)
-GAIN_AT = 103 * KB
-PICKED_AT = ((92 * KB, 12 * KB, 0), (78 * KB, 15 * KB, 13 * KB))
+WB_RAW_AT = ((8 * KB, 6 * KB), (20 * KB, 2 * KB))
+WB_CODES_AT = (24 * KB, WE_RAW_AT[1, 1, 0])
+LAST_CODES_AT = WB_RAW_AT[1][0]
+V_CODES_AT = (26 * KB, 60 * KB)
+PICKED_AT = ((28 * KB, 29 * KB), (22 * KB, 2 * KB))
+GAIN_AT = 41 * KB - 64
 WE_BF_AT = {
-    (0, 0): 93 * KB,
-    (0, 1): 88 * KB,
-    (1, 0): 94 * KB,
-    (1, 1): 97 * KB + KB // 2,
+    (0, 0): (41 * KB, 4 * KB),
+    (0, 1): (54 * KB, 14 * KB),
+    (1, 0): (64 * KB, 4 * KB),
+    (1, 1): (67 * KB + KB // 2, 4 * KB),
 }
-LATE_CODES_AT = 90 * KB
-LOGS_AT = [WE_BF_AT[1, 1] + KB] + [48 * KB + 4 * KB * pair for pair in range(1, 8)]
-EARLY_H_BF_AT = WE_BF_AT[1, 1]
-EARLY_H_CODES_AT = (LOGS_AT[2], LOGS_AT[5])
+LATE_CODES_AT = 58 * KB
+FIRST_ROWS_AT = WE_RAW_AT[1, 0, 0]
+LOGS_AT = [72 * KB + 4 * KB * pair for pair in range(8)]
+SINGLE_LOG_AT = (LOGS_AT[0], WE_BF_AT[1, 1][0] + KB)
+SECOND_CODES_AT = SINGLE_LOG_AT[0]
+EARLY_H_BF_AT = WE_BF_AT[1, 1][0]
+EARLY_H_CODES_AT = (LOGS_AT[3], LOGS_AT[5])
 
 
 def tile_list_barcode_programme_scores_kernel(
@@ -85,7 +90,7 @@ def tile_list_barcode_programme_scores_kernel(
 
         nc.sync.dma_start(
             out=scale_win[0:ROWS, :],
-            in_=tab[0, 512 * T : 544 * T].rearrange("(r b) -> r b", r=ROWS).bitcast(I32),
+            in_=tab[0, 512 * T : 544 * T].rearrange("(row b) -> row b", row=ROWS).bitcast(I32),
         )
         nc.sync.dma_start(offsets[:], offs)
         nc.sync.dma_start(out=wb_rows[0:ROWS, :], in_=wb_scales.rearrange("g q c -> (g q) c").bitcast(I32))
@@ -93,8 +98,9 @@ def tile_list_barcode_programme_scores_kernel(
         wb_raw, we_raw = {}, {}
 
         def load_wb(a):
-            raw = placed([P, W], I32, "wb_raw%d" % a, WB_RAW_AT[a])
-            wb_raw[a] = raw[:].rearrange("p (g b) -> p g b", g=2)
+            at, span = WB_RAW_AT[a]
+            held = placed([P, span // 4], I32, "wb_raw%d" % a, at)
+            wb_raw[a] = held[:, 0:W].rearrange("p (g b) -> p g b", g=2)
             nc.sync.dma_start(
                 out=wb_raw[a],
                 in_=wb_words[:, :, 2 * W * a : 2 * W * (a + 1)].rearrange("g p b -> p g b").bitcast(I32),
@@ -114,7 +120,6 @@ def tile_list_barcode_programme_scores_kernel(
         )
         load_we(0, 0, 0, W)
         load_we(0, 1, 0, HALF)
-        load_we(0, 1, HALF, HALF)
 
         picked_scales = keep.tile([P, S], U8, name="picked_scales", align_bytes=64)
         nc.vector.tensor_copy(picked_scales[:], scale_win[:].bitcast(U8).indirect(offsets[:]))
@@ -126,7 +131,7 @@ def tile_list_barcode_programme_scores_kernel(
         for g in range(2):
             for q in range(4):
                 if (g, q) != (0, 0):
-                    queue = nc.gpsimd if (g, q) >= FIRST_GPSIMD_MOVE else nc.scalar
+                    queue = nc.gpsimd if (g, q) == GPSIMD_MOVE else nc.scalar
                     queue.dma_start(
                         out=planes[g][32 * q : 32 * q + 4, :], in_=planes[0][16 * g + 4 * q : 16 * g + 4 * q + 4, :]
                     )
@@ -142,13 +147,16 @@ def tile_list_barcode_programme_scores_kernel(
             )
 
         permute_wb(0)
+        load_we(0, 1, HALF, HALF)
 
         we_bf, we_codes, we_scales = {}, {}, {}
 
         def round_we(engine, a, g, c0, m0, m1):
             if (a, g) not in we_bf:
-                we_bf[a, g] = placed([P, 4 * W], BF16, "we_bf%d%d" % (a, g), WE_BF_AT[a, g])
-            dst = we_bf[a, g][:].rearrange("p (t m j) -> p m j t", t=4, j=4)[:, c0 // 4 + m0 : c0 // 4 + m1]
+                at, span = WE_BF_AT[a, g]
+                held = placed([P, span // 2], BF16, "we_bf%d%d" % (a, g), at)
+                we_bf[a, g] = held[:, 0 : 4 * W]
+            dst = we_bf[a, g].rearrange("p (t m j) -> p m j t", t=4, j=4)[:, c0 // 4 + m0 : c0 // 4 + m1]
             src = we_raw[a, g, c0][:].rearrange("p j (m t) -> p m j t", t=4)[:, m0:m1]
             if engine == "scalar":
                 nc.scalar.copy(out=dst, in_=src)
@@ -173,16 +181,16 @@ def tile_list_barcode_programme_scores_kernel(
         v_codes = {}
 
         def pick_cells(jt):
-            at, span, skip = PICKED_AT[jt]
+            at, span = PICKED_AT[jt]
             held = placed([P, span // 4], U32, "picked_words%d" % jt, at)
-            picked = held[:, skip // 4 : skip // 4 + W]
+            picked = held[:, 0:W]
             nc.vector.tensor_copy(
                 picked, word_win[:].bitcast(U32).indirect(offsets[:, W // 16 * jt : W // 16 * (jt + 1)])
             )
             return picked
 
         def part_cells(jt, picked):
-            v_codes[jt] = keep.tile([P, 2, 2 * W], U8, name="v_codes%d" % jt, align_bytes=64)
+            v_codes[jt] = placed([P, 2, 2 * W], U8, "v_codes%d" % jt, V_CODES_AT[jt])
             nc.vector.tensor_copy(
                 out=v_codes[jt][:].bitcast(U16), in_=picked.bitcast(U16).rearrange("p (n g) -> p g n", g=2)
             )
@@ -191,18 +199,20 @@ def tile_list_barcode_programme_scores_kernel(
         load_we(1, 0, 0, W)
         gain_sb = placed([P, 2, 4], F32, "gain_sb", GAIN_AT)
         nc.sync.dma_start(out=gain_sb[:], in_=gain.rearrange("(a p t) -> p a t", a=2, t=4))
-        picked = pick_cells(1)
-        round_we("scalar", 0, 0, 0, 0, SCALAR_GROUPS)
-        part_cells(1, picked)
-        load_wb(1)
         load_we(1, 1, 0, W)
-        round_we("vector", 0, 0, 0, SCALAR_GROUPS, W // 4)
-        round_we("vector", 0, 1, 0, 0, HALF // 4)
-        round_we("vector", 0, 1, HALF, 0, HALF // 4)
+        round_we("scalar", 0, 0, 0, 0, SCALAR_GROUPS_FIRST)
+        round_we("vector", 0, 0, 0, SCALAR_GROUPS_FIRST, W // 4)
+        round_we("scalar", 0, 1, 0, 0, HALF // 4)
+        load_wb(1)
+        picked = pick_cells(1)
         quantise_we(0, 0, 0, 2)
-        quantise_we(0, 1, 0, 2)
+        round_we("vector", 0, 1, HALF, 0, HALF // 4 - SCALAR_GROUPS_LAST)
+        round_we("scalar", 0, 1, HALF, HALF // 4 - SCALAR_GROUPS_LAST, HALF // 4)
+        quantise_we(0, 1, 0, 1)
+        quantise_we(0, 1, 1, 2)
         quantise_we(0, 1, 2, 4)
         quantise_we(0, 0, 2, 4, LATE_CODES_AT)
+        part_cells(1, picked)
 
         w2_codes = placed([P, 2, N], I32, "w2_codes", W2_CODES_AT)
         nc.sync.dma_start(out=w2_codes[:], in_=w2_words.rearrange("a p c i -> p a (c i)").bitcast(I32))
@@ -213,12 +223,12 @@ def tile_list_barcode_programme_scores_kernel(
             for q in range(4):
                 nc.sync.dma_start(
                     out=w2_planes[32 * q : 32 * q + 4, :, :],
-                    in_=w2_scales[:, 4 * q : 4 * q + 4, :].rearrange("a r c -> r a c").bitcast(I32),
+                    in_=w2_scales[:, 4 * q : 4 * q + 4, :].rearrange("a s c -> s a c").bitcast(I32),
                 )
 
         units = [(0, 0), (0, 1), (1, 0), (1, 1)]
         h_rows, h_bf, h_codes, h_scales = {}, {}, {}, {}
-        e_ps, b_ps, mags, logs = {}, {}, {}, {}
+        e_ps, b_ps, mags, logs, log_rows = {}, {}, {}, {}, {}
 
         def e_pass(step, g):
             (a, jt), t = units[step // 4], step % 4
@@ -262,17 +272,27 @@ def tile_list_barcode_programme_scores_kernel(
         def logarithm(pair, n0, n1, k0=0, k1=2):
             if pair not in logs:
                 logs[pair] = placed([P, 2, W], F32, "logs%d" % pair, LOGS_AT[pair])
+                for k in range(2):
+                    log_rows[2 * pair + k] = logs[pair][:, k, :]
             nc.scalar.activation(
                 out=logs[pair][:, k0:k1, n0:n1], in_=mags[pair][:, k0:k1, n0:n1], func=ACT.Ln, bias=1.0
             )
 
+        def single_logarithm(step):
+            single = placed([P, W], F32, "log%d" % step, SINGLE_LOG_AT[step])
+            log_rows[step] = single[:]
+            nc.scalar.activation(out=single[:], in_=mags[0][:, step, :], func=ACT.Ln, bias=1.0)
+
         def correct(step, n0, n1):
             u, t = divmod(step, 4)
             if u not in h_rows:
-                h_rows[u] = ring.tile([P, 4, W], BF16, name="h_rows%d" % u, tag="h_rows", align_bytes=64, bufs=3)
+                if u == 0:
+                    h_rows[u] = placed([P, 4, W], BF16, "h_rows0", FIRST_ROWS_AT)
+                else:
+                    h_rows[u] = keep.tile([P, 4, W], BF16, name="h_rows%d" % u, align_bytes=64)
             nc.vector.scalar_tensor_tensor(
                 out=h_rows[u][:, t, n0:n1],
-                in0=logs[step // 2][:, step % 2, n0:n1],
+                in0=log_rows[step][:, n0:n1],
                 scalar=gain_sb[:, units[u][0], t : t + 1],
                 in1=b_ps[step][:, n0:n1],
                 op0=ALU.mult,
@@ -327,12 +347,15 @@ def tile_list_barcode_programme_scores_kernel(
             )
 
         later = {
-            1: [lambda: round_we("vector", 1, 1, 0, 0, W // 4)],
-            2: [lambda: quantise_we(1, 1, 0, 4)],
+            0: [lambda: quantise_we(1, 0, 0, 4, SECOND_CODES_AT)],
+            1: [
+                lambda: round_we("vector", 1, 1, 0, 0, W // 4),
+                lambda: permute_wb(1),
+                lambda: quantise_we(1, 1, 0, 4, LAST_CODES_AT),
+            ],
             3: [lambda: interleave_h("gpsimd", 0, 0, W)],
             5: [load_w2_scales],
-            6: [lambda: quantise_h(0, 0, W)],
-            7: [lambda: interleave_h("gpsimd", 1, 0, W)],
+            7: [lambda: quantise_h(0, 0, W), lambda: interleave_h("gpsimd", 1, 0, W)],
             11: [lambda: interleave_h("vector", 2, 0, W), lambda: quantise_h(1, 0, W), lambda: quantise_h(2, 0, W)],
         }
 
@@ -350,14 +373,16 @@ def tile_list_barcode_programme_scores_kernel(
                 b_pass(step - 2, 1)
 
         round_we("vector", 1, 0, 0, 0, W // 4)
-        permute_wb(1)
-        quantise_we(1, 0, 0, 4)
         e_pass(0, 0)
         e_pass(1, 0)
         products(0)
         products(1)
         for pair in range(6):
-            if pair not in (3, 5):
+            if pair == 0:
+                products(2)
+                single_logarithm(0)
+                single_logarithm(1)
+            elif pair not in (3, 5):
                 products(2 * pair + 2)
                 logarithm(pair, 0, W)
             else:
@@ -383,11 +408,9 @@ def tile_list_barcode_programme_scores_kernel(
         interleave_h("gpsimd", 3, 0, HALF)
         for step in range(12, 16):
             correct(step, HALF, W)
+        interleave_h("vector", 3, HALF, W)
         quantise_h(3, 0, HALF)
-        interleave_h("vector", 3, HALF, HALF + QUARTER)
-        interleave_h("vector", 3, HALF + QUARTER, W)
-        quantise_h(3, HALF, HALF + QUARTER)
-        quantise_h(3, HALF + QUARTER, W)
+        quantise_h(3, HALF, W)
 
         out_v = out.rearrange("(n p) j -> p n j", p=P)
         first = [bank(n, "o_ps%d" % n) for n in range(4)]
@@ -398,33 +421,24 @@ def tile_list_barcode_programme_scores_kernel(
             res = keep.tile([P, W], F32, name="res0_%d" % n)
             nc.scalar.copy(out=res[:], in_=first[n][:])
             nc.sync.dma_start(out=out_v[:, n, 0:W], in_=res[:])
-        parts = [
-            (0, HALF, (4, 5), ("scalar", "scalar")),
-            (HALF, QUARTER, (6,), ("vector",)),
-            (HALF + QUARTER, QUARTER, (7, 0), ("scalar", "vector")),
-        ]
-        part_ps = [[bank(i, "o_ps%d_%d" % (c0, i)) for i in banks] for c0, cells, banks, engines in parts]
 
-        def part_passes(k, a):
-            c0, cells, banks, engines = parts[k]
-            per_bank = 4 // len(banks)
+        second = [[bank(4 + 2 * half + i, "o_ps%d%d" % (half, i)) for i in range(2)] for half in range(2)]
+
+        def second_passes(half, a):
             for n in range(4):
-                i, j = divmod(n, per_bank)
-                dst = part_ps[k][i][:, cells * j : cells * (j + 1)]
-                score_pass(dst, n, 1, a, c0, c0 + cells, (a, j) == (0, 0), (a, j) == (1, per_bank - 1))
+                i, j = divmod(n, 2)
+                dst = second[half][i][:, HALF * j : HALF * (j + 1)]
+                score_pass(dst, n, 1, a, HALF * half, HALF * (half + 1), (a, j) == (0, 0), (a, j) == (1, 1))
 
-        for k in range(len(parts)):
-            part_passes(k, 0)
-        for k, (c0, cells, banks, engines) in enumerate(parts):
-            part_passes(k, 1)
-            per_bank = 4 // len(banks)
-            for i, engine in enumerate(engines):
-                res = keep.tile([P, per_bank, cells], F32, name="res1_%d%d" % (k, i))
-                src = part_ps[k][i][:, 0 : per_bank * cells]
-                if engine == "vector":
-                    nc.vector.tensor_copy(out=res[:].rearrange("p k j -> p (k j)"), in_=src)
+        for half in range(2):
+            second_passes(half, 0)
+        for half in range(2):
+            second_passes(half, 1)
+            for i in range(2):
+                res = keep.tile([P, 2, HALF], F32, name="res1_%d%d" % (half, i))
+                if i == 0:
+                    nc.vector.tensor_copy(out=res[:].rearrange("p k j -> p (k j)"), in_=second[half][i][:])
                 else:
-                    nc.scalar.copy(out=res[:].rearrange("p k j -> p (k j)"), in_=src)
-                nc.sync.dma_start(
-                    out=out_v[:, per_bank * i : per_bank * (i + 1), W + c0 : W + c0 + cells], in_=res[:]
-                )
+                    nc.scalar.copy(out=res[:].rearrange("p k j -> p (k j)"), in_=second[half][i][:])
+                c0 = W + HALF * half
+                nc.sync.dma_start(out=out_v[:, 2 * i : 2 * i + 2, c0 : c0 + HALF], in_=res[:])

@@ -23,7 +23,7 @@ ROWS = 32
 V_AT, WB_AT, PLANE = 0, S, S + H
 KB = 1024
 
-SCALAR_GROUPS_FIRST = 44
+SCALAR_GROUPS_FIRST = 56
 SCALAR_GROUPS_LAST = 20
 GPSIMD_MOVE = (1, 3)
 
@@ -32,14 +32,15 @@ WE_RAW_AT = {
     (0, 1, HALF): 10 * KB,
     (0, 0, 0): 16 * KB,
     (1, 0, 0): 32 * KB + KB // 2,
+    (1, 0, HALF): 36 * KB + KB // 2,
     (1, 1, 0): 45 * KB,
 }
 W2_CODES_AT = 0
 WB_RAW_AT = ((8 * KB, 6 * KB), (20 * KB, 2 * KB))
 WB_CODES_AT = (24 * KB, WE_RAW_AT[1, 1, 0])
 LAST_CODES_AT = WB_RAW_AT[1][0]
-V_CODES_AT = (26 * KB, 60 * KB)
-PICKED_AT = ((28 * KB, 29 * KB), (22 * KB, 2 * KB))
+V_CODES_AT = (26 * KB, 22 * KB)
+PICKED_AT = ((28 * KB, 29 * KB), (28 * KB, 2 * KB))
 GAIN_AT = 41 * KB - 64
 WE_BF_AT = {
     (0, 0): (41 * KB, 4 * KB),
@@ -48,7 +49,7 @@ WE_BF_AT = {
     (1, 1): (67 * KB + KB // 2, 4 * KB),
 }
 LATE_CODES_AT = 58 * KB
-FIRST_ROWS_AT = WE_RAW_AT[1, 0, 0]
+FIRST_ROWS_AT = WE_RAW_AT[1, 0, HALF]
 LOGS_AT = [72 * KB + 4 * KB * pair for pair in range(8)]
 SINGLE_LOG_AT = (LOGS_AT[0], WE_BF_AT[1, 1][0] + KB)
 SECOND_CODES_AT = SINGLE_LOG_AT[0]
@@ -196,7 +197,9 @@ def tile_list_barcode_programme_scores_kernel(
             )
 
         part_cells(0, pick_cells(0))
-        load_we(1, 0, 0, W)
+        picked = pick_cells(1)
+        load_we(1, 0, 0, HALF)
+        load_we(1, 0, HALF, HALF)
         gain_sb = placed([P, 2, 4], F32, "gain_sb", GAIN_AT)
         nc.sync.dma_start(out=gain_sb[:], in_=gain.rearrange("(a p t) -> p a t", a=2, t=4))
         load_we(1, 1, 0, W)
@@ -204,7 +207,7 @@ def tile_list_barcode_programme_scores_kernel(
         round_we("vector", 0, 0, 0, SCALAR_GROUPS_FIRST, W // 4)
         round_we("scalar", 0, 1, 0, 0, HALF // 4)
         load_wb(1)
-        picked = pick_cells(1)
+        part_cells(1, picked)
         quantise_we(0, 0, 0, 2)
         round_we("vector", 0, 1, HALF, 0, HALF // 4 - SCALAR_GROUPS_LAST)
         round_we("scalar", 0, 1, HALF, HALF // 4 - SCALAR_GROUPS_LAST, HALF // 4)
@@ -212,7 +215,6 @@ def tile_list_barcode_programme_scores_kernel(
         quantise_we(0, 1, 1, 2)
         quantise_we(0, 1, 2, 4)
         quantise_we(0, 0, 2, 4, LATE_CODES_AT)
-        part_cells(1, picked)
 
         w2_codes = placed([P, 2, N], I32, "w2_codes", W2_CODES_AT)
         nc.sync.dma_start(out=w2_codes[:], in_=w2_words.rearrange("a p c i -> p a (c i)").bitcast(I32))
@@ -372,16 +374,17 @@ def tile_list_barcode_programme_scores_kernel(
                 b_pass(step - 2, 0)
                 b_pass(step - 2, 1)
 
-        round_we("vector", 1, 0, 0, 0, W // 4)
+        round_we("vector", 1, 0, 0, 0, HALF // 4)
+        round_we("vector", 1, 0, HALF, 0, HALF // 4)
         e_pass(0, 0)
         e_pass(1, 0)
         products(0)
         products(1)
         for pair in range(6):
             if pair == 0:
-                products(2)
                 single_logarithm(0)
                 single_logarithm(1)
+                products(2)
             elif pair not in (3, 5):
                 products(2 * pair + 2)
                 logarithm(pair, 0, W)

@@ -24,12 +24,14 @@ V_AT, WB_AT, PLANE = 0, S, S + H
 KB = 1024
 
 SCALAR_GROUPS_FIRST = 56
-SCALAR_GROUPS_LAST = 20
+SCALAR_GROUPS_MIDDLE = 32
+SCALAR_GROUPS_LAST = 10
+CUT = 3 * W // 4
 GPSIMD_MOVE = (1, 3)
 
 WE_RAW_AT = {
     (0, 1, 0): 0,
-    (0, 1, HALF): 10 * KB,
+    (0, 1, CUT): 10 * KB,
     (0, 0, 0): 16 * KB,
     (1, 0, 0): 32 * KB + KB // 2,
     (1, 0, HALF): 36 * KB + KB // 2,
@@ -120,7 +122,7 @@ def tile_list_barcode_programme_scores_kernel(
             out=word_win[:], in_=tab[0, 0 : 512 * T].rearrange("(p b) -> p b", p=P).bitcast(I32)
         )
         load_we(0, 0, 0, W)
-        load_we(0, 1, 0, HALF)
+        load_we(0, 1, 0, CUT)
 
         picked_scales = keep.tile([P, S], U8, name="picked_scales", align_bytes=64)
         nc.vector.tensor_copy(picked_scales[:], scale_win[:].bitcast(U8).indirect(offsets[:]))
@@ -148,7 +150,7 @@ def tile_list_barcode_programme_scores_kernel(
             )
 
         permute_wb(0)
-        load_we(0, 1, HALF, HALF)
+        load_we(0, 1, CUT, W - CUT)
 
         we_bf, we_codes, we_scales = {}, {}, {}
 
@@ -205,12 +207,13 @@ def tile_list_barcode_programme_scores_kernel(
         load_we(1, 1, 0, W)
         round_we("scalar", 0, 0, 0, 0, SCALAR_GROUPS_FIRST)
         round_we("vector", 0, 0, 0, SCALAR_GROUPS_FIRST, W // 4)
-        round_we("scalar", 0, 1, 0, 0, HALF // 4)
+        round_we("scalar", 0, 1, 0, 0, SCALAR_GROUPS_MIDDLE)
         load_wb(1)
         part_cells(1, picked)
         quantise_we(0, 0, 0, 2)
-        round_we("vector", 0, 1, HALF, 0, HALF // 4 - SCALAR_GROUPS_LAST)
-        round_we("scalar", 0, 1, HALF, HALF // 4 - SCALAR_GROUPS_LAST, HALF // 4)
+        round_we("vector", 0, 1, 0, SCALAR_GROUPS_MIDDLE, CUT // 4)
+        round_we("vector", 0, 1, CUT, 0, (W - CUT) // 4 - SCALAR_GROUPS_LAST)
+        round_we("scalar", 0, 1, CUT, (W - CUT) // 4 - SCALAR_GROUPS_LAST, (W - CUT) // 4)
         quantise_we(0, 1, 0, 1)
         quantise_we(0, 1, 1, 2)
         quantise_we(0, 1, 2, 4)

@@ -38,9 +38,9 @@ WE_RAW_AT = {
     (1, 1, 0): 45 * KB,
 }
 W2_CODES_AT = 0
-WB_RAW_AT = ((8 * KB, 6 * KB), (20 * KB, 2 * KB))
+WB_RAW_AT = ((8 * KB, 6 * KB), (16 * KB, 2 * KB))
 WB_CODES_AT = (24 * KB, WE_RAW_AT[1, 1, 0])
-LAST_CODES_AT = WB_RAW_AT[1][0]
+LAST_CODES_AT = WE_RAW_AT[1, 1, 0] + 2 * KB
 V_CODES_AT = (26 * KB, 22 * KB)
 PICKED_AT = ((28 * KB, 29 * KB), (28 * KB, 2 * KB))
 GAIN_AT = 41 * KB - 64
@@ -55,7 +55,7 @@ FIRST_ROWS_AT = WE_RAW_AT[1, 0, HALF]
 LOGS_AT = [72 * KB + 4 * KB * pair for pair in range(8)]
 SINGLE_LOG_AT = (LOGS_AT[0], WE_BF_AT[1, 1][0] + KB)
 SECOND_CODES_AT = SINGLE_LOG_AT[0]
-EARLY_H_BF_AT = WE_BF_AT[1, 1][0]
+EARLY_H_BF_AT = WB_RAW_AT[1][0]
 EARLY_H_CODES_AT = (LOGS_AT[3], LOGS_AT[5])
 
 
@@ -238,7 +238,7 @@ def tile_list_barcode_programme_scores_kernel(
         def e_pass(step, g):
             (a, jt), t = units[step // 4], step % 4
             if g == 0:
-                e_ps[step] = bank(t, "e_ps%d" % step)
+                e_ps[step] = bank(step % 3 if step else 7, "e_ps%d" % step)
             nc.tensor.matmul_mx(
                 out=e_ps[step][:],
                 lhsT=we_codes[a, g, t].bitcast(FP8X4),
@@ -252,7 +252,7 @@ def tile_list_barcode_programme_scores_kernel(
         def b_pass(step, g):
             (a, jt), t = units[step // 4], step % 4
             if g == 0:
-                b_ps[step] = bank(4 + t, "b_ps%d" % step)
+                b_ps[step] = bank(3 + step % 5, "b_ps%d" % step)
             c0 = WB_AT + W * a + P * t
             nc.tensor.matmul_mx(
                 out=b_ps[step][:],
@@ -353,12 +353,9 @@ def tile_list_barcode_programme_scores_kernel(
 
         later = {
             0: [lambda: quantise_we(1, 0, 0, 4, SECOND_CODES_AT)],
-            1: [
-                lambda: round_we("vector", 1, 1, 0, 0, W // 4),
-                lambda: permute_wb(1),
-                lambda: quantise_we(1, 1, 0, 4, LAST_CODES_AT),
-            ],
-            3: [lambda: interleave_h("gpsimd", 0, 0, W)],
+            1: [lambda: round_we("vector", 1, 1, 0, 0, W // 4)],
+            2: [lambda: quantise_we(1, 1, 0, 4, LAST_CODES_AT)],
+            3: [lambda: permute_wb(1), lambda: interleave_h("gpsimd", 0, 0, W)],
             5: [load_w2_scales],
             7: [lambda: quantise_h(0, 0, W), lambda: interleave_h("gpsimd", 1, 0, W)],
             11: [lambda: interleave_h("vector", 2, 0, W), lambda: quantise_h(1, 0, W), lambda: quantise_h(2, 0, W)],
@@ -373,9 +370,9 @@ def tile_list_barcode_programme_scores_kernel(
                 e_pass(step, 0)
             e_pass(step, 1)
             magnitude(step)
-            if step >= 6:
-                b_pass(step - 2, 0)
-                b_pass(step - 2, 1)
+            if step >= 5:
+                b_pass(step - 1, 0)
+                b_pass(step - 1, 1)
 
         round_we("vector", 1, 0, 0, 0, HALF // 4)
         round_we("vector", 1, 0, HALF, 0, HALF // 4)
@@ -403,9 +400,8 @@ def tile_list_barcode_programme_scores_kernel(
         products(14)
         logarithm(6, 0, HALF)
         products(15)
-        for step in (14, 15):
-            b_pass(step, 0)
-            b_pass(step, 1)
+        b_pass(15, 0)
+        b_pass(15, 1)
         logarithm(7, 0, HALF)
         logarithm(6, HALF, W)
         logarithm(7, HALF, W)
@@ -419,7 +415,7 @@ def tile_list_barcode_programme_scores_kernel(
         quantise_h(3, HALF, W)
 
         out_v = out.rearrange("(n p) j -> p n j", p=P)
-        first = [bank(n, "o_ps%d" % n) for n in range(4)]
+        first = [bank(i, "o_ps%d" % n) for n, i in enumerate((4, 1, 2, 0))]
         for a in range(2):
             for n in range(4):
                 score_pass(first[n][:], n, 0, a, 0, W, a == 0, a == 1)
@@ -428,7 +424,7 @@ def tile_list_barcode_programme_scores_kernel(
             nc.scalar.copy(out=res[:], in_=first[n][:])
             nc.sync.dma_start(out=out_v[:, n, 0:W], in_=res[:])
 
-        second = [[bank(4 + 2 * half + i, "o_ps%d%d" % (half, i)) for i in range(2)] for half in range(2)]
+        second = [[bank(3 + (12 + 2 * half + i) % 5, "o_ps%d%d" % (half, i)) for i in range(2)] for half in range(2)]
 
         def second_passes(half, a):
             for n in range(4):

from contextlib import ExitStack

import concourse.mybir as mybir

K, T, S, H, N = 1024, 4096, 1024, 1024, 512
FLOPS = 2 * (2 * K * H * S + H * N * S)

F32 = mybir.dt.float32
BF16 = mybir.dt.bfloat16
I32 = mybir.dt.int32
U32 = mybir.dt.uint32
U16 = mybir.dt.uint16
U8 = mybir.dt.uint8
FP8X4 = mybir.dt.float8_e4m3fn_x4
FP4X4 = mybir.dt.float4_e2m1fn_x4
ACT = mybir.ActivationFunctionType
ALU = mybir.AluOpType

P = 128
W = 512
HALF = W // 2
ROWS = 32
V_AT, WB_AT, PLANE = 0, S, S + H
KB = 1024

SCALAR_GROUPS_FIRST = 56
SCALAR_GROUPS_MIDDLE = 32
SCALAR_GROUPS_LAST = 10
CUT = 3 * W // 4
GPSIMD_MOVE = (1, 3)

WE_RAW_AT = {
    (0, 1, 0): 0,
    (0, 1, CUT): 10 * KB,
    (0, 0, 0): 16 * KB,
    (1, 0, 0): 32 * KB + KB // 2,
    (1, 0, HALF): 36 * KB + KB // 2,
    (1, 1, 0): 45 * KB,
}
W2_CODES_AT = 0
WB_RAW_AT = ((8 * KB, 6 * KB), (16 * KB, 2 * KB))
WB_CODES_AT = (24 * KB, WE_RAW_AT[1, 1, 0])
LAST_CODES_AT = WE_RAW_AT[1, 1, 0] + 2 * KB
V_CODES_AT = (26 * KB, 22 * KB)
PICKED_AT = ((28 * KB, 29 * KB), (28 * KB, 2 * KB))
GAIN_AT = 41 * KB - 64
WE_BF_AT = {
    (0, 0): (41 * KB, 4 * KB),
    (0, 1): (54 * KB, 14 * KB),
    (1, 0): (64 * KB, 4 * KB),
    (1, 1): (67 * KB + KB // 2, 4 * KB),
}
LATE_CODES_AT = 58 * KB
FIRST_ROWS_AT = WE_RAW_AT[1, 0, HALF]
LOGS_AT = [72 * KB + 4 * KB * pair for pair in range(8)]
SINGLE_LOG_AT = (LOGS_AT[0], WE_BF_AT[1, 1][0] + KB)
SECOND_CODES_AT = SINGLE_LOG_AT[0]
EARLY_H_BF_AT = WB_RAW_AT[1][0]
EARLY_H_CODES_AT = (LOGS_AT[3], LOGS_AT[5])


def tile_list_barcode_programme_scores_kernel(
    tc, tab, offs, we, wb_words, wb_scales, gain, w2_words, w2_scales, out
):
    nc = tc.nc
    with ExitStack() as ctx:
        keep = ctx.enter_context(tc.tile_pool(name="keep", bufs=1))
        ring = ctx.enter_context(tc.tile_pool(name="ring", bufs=2))
        reuse = ctx.enter_context(tc.tile_pool(name="reuse", bufs=1))
        psum = ctx.enter_context(tc.psum_pool(name="psum", bufs=1))

        def bank(i, name):
            return psum.tile([P, W], F32, name=name, tag="bank%d" % i)

        def placed(shape, dtype, name, at):
            return reuse.tile(shape, dtype, name=name, align_bytes=64, offset=at)

        offsets = keep.tile([P, S // 16], U16, name="offsets")
        scale_win = keep.tile([P, T // 4], I32, name="scale_win", align_bytes=64)
        word_win = keep.tile([P, T], I32, name="word_win", align_bytes=64)
        planes = [keep.tile([P, PLANE // 4], I32, name="plane%d" % g, align_bytes=64) for g in range(2)]
        wb_rows = keep.tile([P, H // 4], I32, name="wb_rows", align_bytes=64)
        one = keep.tile([P, 1], F32, name="one")
        zero = keep.tile([P, 1], F32, name="zero")

        nc.vector.memset(one[:], 1.0)
        nc.scalar.activation(out=zero[:], in_=one[:], func=ACT.Ln)
        nc.vector.memset(scale_win[32:64, :], 0)
        nc.vector.memset(scale_win[64:128, :], 0)
        nc.vector.memset(wb_rows[32:64, :], 0)
        nc.vector.memset(wb_rows[64:128, :], 0)
        nc.vector.memset(planes[1][:], 0)

        nc.sync.dma_start(
            out=scale_win[0:ROWS, :],
            in_=tab[0, 512 * T : 544 * T].rearrange("(row b) -> row b", row=ROWS).bitcast(I32),
        )
        nc.sync.dma_start(offsets[:], offs)
        nc.sync.dma_start(out=wb_rows[0:ROWS, :], in_=wb_scales.rearrange("g q c -> (g q) c").bitcast(I32))

        wb_raw, we_raw = {}, {}

        def load_wb(a):
            at, span = WB_RAW_AT[a]
            held = placed([P, span // 4], I32, "wb_raw%d" % a, at)
            wb_raw[a] = held[:, 0:W].rearrange("p (g b) -> p g b", g=2)
            nc.sync.dma_start(
                out=wb_raw[a],
                in_=wb_words[:, :, 2 * W * a : 2 * W * (a + 1)].rearrange("g p b -> p g b").bitcast(I32),
            )

        def load_we(a, g, c0, cw):
            raw = placed([P, 4, cw], F32, "we_raw%d%d_%d" % (a, g, c0), WE_RAW_AT[a, g, c0])
            nc.sync.dma_start(
                out=raw[:],
                in_=we[W * g : W * (g + 1), W * a + c0 : W * a + c0 + cw].rearrange("(p j) c -> p j c", j=4),
            )
            we_raw[a, g, c0] = raw

        load_wb(0)
        nc.sync.dma_start(
            out=word_win[:], in_=tab[0, 0 : 512 * T].rearrange("(p b) -> p b", p=P).bitcast(I32)
        )
        load_we(0, 0, 0, W)
        load_we(0, 1, 0, CUT)

        picked_scales = keep.tile([P, S], U8, name="picked_scales", align_bytes=64)
        nc.vector.tensor_copy(picked_scales[:], scale_win[:].bitcast(U8).indirect(offsets[:]))
        nc.vector.tensor_copy(
            out=planes[0][:].bitcast(U8)[:, WB_AT:PLANE].rearrange("p (a t m) -> p a t m", a=2, t=4),
            in_=wb_rows[:].bitcast(U8).rearrange("p (a m t) -> p a t m", a=2, t=4),
        )
        nc.vector.tensor_copy(out=planes[0][:, 0 : S // 4], in_=picked_scales[:].bitcast(I32))
        for g in range(2):
            for q in range(4):
                if (g, q) != (0, 0):
                    queue = nc.gpsimd if (g, q) == GPSIMD_MOVE else nc.scalar
                    queue.dma_start(
                        out=planes[g][32 * q : 32 * q + 4, :], in_=planes[0][16 * g + 4 * q : 16 * g + 4 * q + 4, :]
                    )
        plane_bytes = [pl[:].bitcast(U8) for pl in planes]

        wb_codes = {}

        def permute_wb(a):
            wb_codes[a] = placed([P, 2, 2 * W], U8, "wb_codes%d" % a, WB_CODES_AT[a])
            nc.vector.tensor_copy(
                out=wb_codes[a][:].bitcast(U16).rearrange("p g (t m) -> p g t m", t=4),
                in_=wb_raw[a].bitcast(U16).rearrange("p g (m t) -> p g t m", t=4),
            )

        permute_wb(0)
        load_we(0, 1, CUT, W - CUT)

        we_bf, we_codes, we_scales = {}, {}, {}

        def round_we(engine, a, g, c0, m0, m1):
            if (a, g) not in we_bf:
                at, span = WE_BF_AT[a, g]
                held = placed([P, span // 2], BF16, "we_bf%d%d" % (a, g), at)
                we_bf[a, g] = held[:, 0 : 4 * W]
            dst = we_bf[a, g].rearrange("p (t m j) -> p m j t", t=4, j=4)[:, c0 // 4 + m0 : c0 // 4 + m1]
            src = we_raw[a, g, c0][:].rearrange("p j (m t) -> p m j t", t=4)[:, m0:m1]
            if engine == "scalar":
                nc.scalar.copy(out=dst, in_=src)
            else:
                nc.vector.tensor_copy(out=dst, in_=src)

        we_planes = [keep.tile([P, 2, W], U8, name="we_planes%d" % a, align_bytes=64) for a in range(2)]

        def quantise_we(a, g, t0, t1, at=None):
            name = "%d%d%d" % (a, g, t0)
            width = P * (t1 - t0)
            if at is None:
                codes = keep.tile([P, width], U32, name="we_codes" + name, align_bytes=64)
            else:
                codes = placed([P, width], U32, "we_codes" + name, at)
            scales = we_planes[a][:, g, P * t0 : P * t1]
            nc.vector.quantize_mx(out=codes[:].bitcast(FP8X4), scales=scales, in_=we_bf[a, g][:, W * t0 : W * t1])
            for t in range(t0, t1):
                we_codes[a, g, t] = codes[:, P * (t - t0) : P * (t - t0 + 1)]
                we_scales[a, g, t] = scales[:, P * (t - t0) : P * (t - t0 + 1)]

        v_codes = {}

        def pick_cells(jt):
            at, span = PICKED_AT[jt]
            held = placed([P, span // 4], U32, "picked_words%d" % jt, at)
            picked = held[:, 0:W]
            nc.vector.tensor_copy(
                picked, word_win[:].bitcast(U32).indirect(offsets[:, W // 16 * jt : W // 16 * (jt + 1)])
            )
            return picked

        def part_cells(jt, picked):
            v_codes[jt] = placed([P, 2, 2 * W], U8, "v_codes%d" % jt, V_CODES_AT[jt])
            nc.vector.tensor_copy(
                out=v_codes[jt][:].bitcast(U16), in_=picked.bitcast(U16).rearrange("p (n g) -> p g n", g=2)
            )

        part_cells(0, pick_cells(0))
        picked = pick_cells(1)
        load_we(1, 0, 0, HALF)
        load_we(1, 0, HALF, HALF)
        gain_sb = placed([P, 2, 4], F32, "gain_sb", GAIN_AT)
        nc.sync.dma_start(out=gain_sb[:], in_=gain.rearrange("(a p t) -> p a t", a=2, t=4))
        load_we(1, 1, 0, W)
        round_we("scalar", 0, 0, 0, 0, SCALAR_GROUPS_FIRST)
        round_we("vector", 0, 0, 0, SCALAR_GROUPS_FIRST, W // 4)
        round_we("scalar", 0, 1, 0, 0, SCALAR_GROUPS_MIDDLE)
        load_wb(1)
        part_cells(1, picked)
        quantise_we(0, 0, 0, 2)
        round_we("vector", 0, 1, 0, SCALAR_GROUPS_MIDDLE, CUT // 4)
        round_we("vector", 0, 1, CUT, 0, (W - CUT) // 4 - SCALAR_GROUPS_LAST)
        round_we("scalar", 0, 1, CUT, (W - CUT) // 4 - SCALAR_GROUPS_LAST, (W - CUT) // 4)
        quantise_we(0, 1, 0, 1)
        quantise_we(0, 1, 1, 2)
        quantise_we(0, 1, 2, 4)
        quantise_we(0, 0, 2, 4, LATE_CODES_AT)

        w2_codes = placed([P, 2, N], I32, "w2_codes", W2_CODES_AT)
        nc.sync.dma_start(out=w2_codes[:], in_=w2_words.rearrange("a p c i -> p a (c i)").bitcast(I32))
        w2_planes = we_planes[0][:].bitcast(I32)
        w2_plane_bytes = we_planes[0][:]

        def load_w2_scales():
            for q in range(4):
                nc.sync.dma_start(
                    out=w2_planes[32 * q : 32 * q + 4, :, :],
                    in_=w2_scales[:, 4 * q : 4 * q + 4, :].rearrange("a s c -> s a c").bitcast(I32),
                )

        units = [(0, 0), (0, 1), (1, 0), (1, 1)]
        h_rows, h_bf, h_codes, h_scales = {}, {}, {}, {}
        e_ps, b_ps, mags, logs, log_rows = {}, {}, {}, {}, {}

        def e_pass(step, g):
            (a, jt), t = units[step // 4], step % 4
            if g == 0:
                e_ps[step] = bank(step % 3 if step else 7, "e_ps%d" % step)
            nc.tensor.matmul_mx(
                out=e_ps[step][:],
                lhsT=we_codes[a, g, t].bitcast(FP8X4),
                lhsT_scale=we_scales[a, g, t],
                rhs=v_codes[jt][:, g, :].bitcast(FP4X4),
                rhs_scale=plane_bytes[g][:, V_AT + W * jt : V_AT + W * (jt + 1)],
                start=(g == 0),
                stop=(g == 1),
            )

        def b_pass(step, g):
            (a, jt), t = units[step // 4], step % 4
            if g == 0:
                b_ps[step] = bank(3 + step % 5, "b_ps%d" % step)
            c0 = WB_AT + W * a + P * t
            nc.tensor.matmul_mx(
                out=b_ps[step][:],
                lhsT=wb_codes[a][:, g, 2 * P * t : 2 * P * (t + 1)].bitcast(FP4X4),
                lhsT_scale=plane_bytes[g][:, c0 : c0 + P],
                rhs=v_codes[jt][:, g, :].bitcast(FP4X4),
                rhs_scale=plane_bytes[g][:, V_AT + W * jt : V_AT + W * (jt + 1)],
                start=(g == 0),
                stop=(g == 1),
            )

        def magnitude(step):
            if step % 2 == 0:
                mags[step // 2] = ring.tile([P, 2, W], F32, name="mag%d" % step, tag="mag", bufs=3)
            nc.scalar.activation(
                out=mags[step // 2][:, step % 2, :],
                in_=e_ps[step][:],
                func=ACT.Abs,
                bias=zero[:] if step == 0 else 0.0,
            )

        def logarithm(pair, n0, n1, k0=0, k1=2):
            if pair not in logs:
                logs[pair] = placed([P, 2, W], F32, "logs%d" % pair, LOGS_AT[pair])
                for k in range(2):
                    log_rows[2 * pair + k] = logs[pair][:, k, :]
            nc.scalar.activation(
                out=logs[pair][:, k0:k1, n0:n1], in_=mags[pair][:, k0:k1, n0:n1], func=ACT.Ln, bias=1.0
            )

        def single_logarithm(step):
            single = placed([P, W], F32, "log%d" % step, SINGLE_LOG_AT[step])
            log_rows[step] = single[:]
            nc.scalar.activation(out=single[:], in_=mags[0][:, step, :], func=ACT.Ln, bias=1.0)

        def correct(step, n0, n1):
            u, t = divmod(step, 4)
            if u not in h_rows:
                if u == 0:
                    h_rows[u] = placed([P, 4, W], BF16, "h_rows0", FIRST_ROWS_AT)
                else:
                    h_rows[u] = keep.tile([P, 4, W], BF16, name="h_rows%d" % u, align_bytes=64)
            nc.vector.scalar_tensor_tensor(
                out=h_rows[u][:, t, n0:n1],
                in0=log_rows[step][:, n0:n1],
                scalar=gain_sb[:, units[u][0], t : t + 1],
                in1=b_ps[step][:, n0:n1],
                op0=ALU.mult,
                op1=ALU.subtract,
            )

        def interleave_h(engine, u, n0, n1):
            if u not in h_bf:
                if u < 2:
                    h_bf[u] = placed([P, 4 * W], BF16, "h_bf%d" % u, EARLY_H_BF_AT)
                else:
                    h_bf[u] = ring.tile([P, 4 * W], BF16, name="h_bf%d" % u, tag="h_bf", align_bytes=64)
            dst, src = h_bf[u][:, 4 * n0 : 4 * n1], h_rows[u][:, :, n0:n1]
            if engine == "gpsimd":
                nc.gpsimd.tensor_scalar(
                    out=dst.rearrange("p (n t) -> p n t", t=4),
                    in0=src.rearrange("p t n -> p n t"),
                    scalar1=1.0,
                    scalar2=0.0,
                    op0=ALU.mult,
                    op1=ALU.add,
                )
            else:
                nc.vector.tensor_copy(
                    out=dst.rearrange("p (c i t) -> p c t i", i=4, t=4),
                    in_=src.rearrange("p t (c i) -> p c t i", i=4),
                )

        def quantise_h(u, n0, n1):
            if u not in h_codes:
                if u < 2:
                    h_codes[u] = placed([P, W], U32, "h_codes%d" % u, EARLY_H_CODES_AT[u])
                else:
                    h_codes[u] = keep.tile([P, W], U32, name="h_codes%d" % u, align_bytes=64)
                h_scales[u] = keep.tile([P, W], U8, name="h_scales%d" % u, align_bytes=64)
            nc.vector.quantize_mx(
                out=h_codes[u][:, n0:n1].bitcast(FP8X4),
                scales=h_scales[u][:, n0:n1],
                in_=h_bf[u][:, 4 * n0 : 4 * n1],
            )

        def score_pass(dst, n, jt, a, n0, n1, start, stop):
            u = units.index((a, jt))
            nc.tensor.matmul_mx(
                out=dst,
                lhsT=w2_codes[:, a, P * n : P * (n + 1)].bitcast(FP8X4),
                lhsT_scale=w2_plane_bytes[:, a, P * n : P * (n + 1)],
                rhs=h_codes[u][:, n0:n1].bitcast(FP8X4),
                rhs_scale=h_scales[u][:, n0:n1],
                start=start,
                stop=stop,
            )

        later = {
            0: [lambda: quantise_we(1, 0, 0, 4, SECOND_CODES_AT)],
            1: [lambda: round_we("vector", 1, 1, 0, 0, W // 4)],
            2: [lambda: quantise_we(1, 1, 0, 4, LAST_CODES_AT)],
            3: [lambda: permute_wb(1), lambda: interleave_h("gpsimd", 0, 0, W)],
            5: [load_w2_scales],
            7: [lambda: quantise_h(0, 0, W), lambda: interleave_h("gpsimd", 1, 0, W)],
            11: [lambda: interleave_h("vector", 2, 0, W), lambda: quantise_h(1, 0, W), lambda: quantise_h(2, 0, W)],
        }

        for g in range(2):
            for t in range(4):
                b_pass(t, g)

        def products(step):
            if step >= 2:
                e_pass(step, 0)
            e_pass(step, 1)
            magnitude(step)
            if step >= 5:
                b_pass(step - 1, 0)
                b_pass(step - 1, 1)

        round_we("vector", 1, 0, 0, 0, HALF // 4)
        round_we("vector", 1, 0, HALF, 0, HALF // 4)
        e_pass(0, 0)
        e_pass(1, 0)
        products(0)
        products(1)
        for pair in range(6):
            if pair == 0:
                single_logarithm(0)
                single_logarithm(1)
                products(2)
            elif pair not in (3, 5):
                products(2 * pair + 2)
                logarithm(pair, 0, W)
            else:
                logarithm(pair, 0, W, 0, 1)
                logarithm(pair, 0, W, 1, 2)
                products(2 * pair + 2)
            products(2 * pair + 3)
            for step in (2 * pair, 2 * pair + 1):
                correct(step, 0, W)
                for job in later.get(step, []):
                    job()
        products(14)
        logarithm(6, 0, HALF)
        products(15)
        b_pass(15, 0)
        b_pass(15, 1)
        logarithm(7, 0, HALF)
        logarithm(6, HALF, W)
        logarithm(7, HALF, W)
        for step in range(12, 16):
            correct(step, 0, HALF)
        interleave_h("gpsimd", 3, 0, HALF)
        for step in range(12, 16):
            correct(step, HALF, W)
        interleave_h("vector", 3, HALF, W)
        quantise_h(3, 0, HALF)
        quantise_h(3, HALF, W)

        out_v = out.rearrange("(n p) j -> p n j", p=P)
        first = [bank(i, "o_ps%d" % n) for n, i in enumerate((4, 1, 2, 0))]
        for a in range(2):
            for n in range(4):
                score_pass(first[n][:], n, 0, a, 0, W, a == 0, a == 1)
        for n in range(4):
            res = keep.tile([P, W], F32, name="res0_%d" % n)
            nc.scalar.copy(out=res[:], in_=first[n][:])
            nc.sync.dma_start(out=out_v[:, n, 0:W], in_=res[:])

        second = [[bank(3 + (12 + 2 * half + i) % 5, "o_ps%d%d" % (half, i)) for i in range(2)] for half in range(2)]

        def second_passes(half, a):
            for n in range(4):
                i, j = divmod(n, 2)
                dst = second[half][i][:, HALF * j : HALF * (j + 1)]
                score_pass(dst, n, 1, a, HALF * half, HALF * (half + 1), (a, j) == (0, 0), (a, j) == (1, 1))

        for half in range(2):
            second_passes(half, 0)
        for half in range(2):
            second_passes(half, 1)
            for i in range(2):
                res = keep.tile([P, 2, HALF], F32, name="res1_%d%d" % (half, i))
                if i == 0:
                    nc.vector.tensor_copy(out=res[:].rearrange("p k j -> p (k j)"), in_=second[half][i][:])
                else:
                    nc.scalar.copy(out=res[:].rearrange("p k j -> p (k j)"), in_=second[half][i][:])
                c0 = W + HALF * half
                nc.sync.dma_start(out=out_v[:, 2 * i : 2 * i + 2, c0 : c0 + HALF], in_=res[:])
